import numpy as np, ml_dtypes
CORES = [6,15,38,47]
N = 4
import mx_ref
BF = ml_dtypes.bfloat16
def entries(a):
    return np.ascontiguousarray(a.T).reshape(-1)
def table(e):
    return np.ascontiguousarray(np.reshape(e, (-1, 16)).T).astype(np.int32)
def pick(q, e):
    c = np.concatenate([q[0].reshape(128, -1, 4), np.zeros((128, 1, 4), np.uint8)], axis=1); s = np.concatenate([q[1], np.ones((16, 1), np.uint8)], axis=1)
    return (np.ascontiguousarray(c[:, e].reshape(128, -1)), np.ascontiguousarray(s[:, e]))
def join(*qs):
    return (np.concatenate([q[0] for q in qs], axis=1), np.concatenate([q[1] for q in qs], axis=1))
def put(q, e, v):
    c, s = q[0].reshape(128, -1, 4).copy(), q[1].copy(); c[:, e] = v[0].reshape(128, -1, 4); s[:, e] = v[1]
    return (c.reshape(128, -1), s)
def pk(c, s):
    return (np.ascontiguousarray(c), mx_ref.live(s))
def emit(q):
    return q[0], q[1]
def decode(q):
    o = []
    for b in range(4):
        e = np.zeros((128, 128, 4), np.float32); e[np.arange(128), np.arange(128), b] = 1
        o.append(mx_ref.matmul(mx_ref.quantize(e.reshape(128, 512).astype(BF)), q))
    return np.stack(o, axis=2).reshape(128, -1)
def cut(t, i, w=512):
    return t[:, w * i:w * i + w]
def f(rng, *shape):
    return mx_ref.flush((rng.standard_normal(shape, dtype=np.float32) * np.exp2(rng.integers(-2, 3, shape[:-1] + (1,)))).astype(BF))
def wide(rng, *shape, cols=0):
    v = rng.standard_normal(shape, dtype=np.float32) * np.exp2(rng.integers(-12, 13, shape)).astype(np.float32)
    if cols: v *= np.repeat(np.exp2(rng.integers(-cols, cols + 1, shape[:-2] + (1, shape[-1] // 4))) * (rng.random(shape[:-2] + (1, shape[-1] // 4)) > 0.0625), 4, axis=-1).astype(np.float32)
    return mx_ref.flush(v.astype(BF))
P, S, K, R, B, M, O = 384, 32, 32, 4, 60, 3, 2
def big(v):
    v = np.array(v).astype(np.float32)
    v[np.abs(v) < np.float32(2.0 ** -16)] = 0
    return v.astype(BF)
def link(adj, a, b):
    a, b = int(a), int(b)
    if a != b and len(adj[a]) < M and len(adj[b]) < M and b not in adj[a]:
        adj[a].append(b)
        adj[b].append(a)
def inner(rng, adj, e):
    for t in range(2 * M):
        a = rng.permutation(e)
        for i in range(0, a.size - 1, 2): link(adj, a[i], a[i + 1])
def across(rng, adj, ranks):
    for r in ranks:
        for q in ranks:
            if r < q:
                a, c = P * r + rng.permutation(P), P * q + rng.permutation(P)
                n = int(rng.integers(B // 2, B + 1))
                for i in range(n):
                    link(adj, a[i], c[i])
                    if i % 3 == 0: link(adj, a[i], c[(i + 1) % n])
def graph(rng):
    adj = [[] for a in range(N * P)]
    across(rng, adj, range(N))
    for r in range(N): inner(rng, adj, np.arange(P * r, P * r + P))
    return adj
def seeds(rng):
    return np.stack([rng.permutation(P)[:S] for r in range(N)])
def lists(rng, adj, s, late=False):
    at = np.argsort(rng.random((N * P, M)), axis=1)
    seed = np.zeros(N * P, bool)
    for r in range(N): seed[P * r + s[r]] = True
    n = np.full((N, M, P), -1)
    for a in range(N * P):
        k, e = at[a, :len(adj[a])], adj[a]
        if late: k, e = np.sort(k), sorted(e, key=lambda c: bool(seed[c]))
        for i, c in zip(k, e): n[a // P, i, a % P] = c
    return {"nb": np.stack([table(v.reshape(-1)) for v in n]), "sd": np.stack([table(v) for v in s])}
def plain(rng):
    return {"x": big(f(rng, N, 128, 4 * P)), "w": f(rng, N, 128, 512 * O)}
def setup_inputs(rng):
    return {**plain(rng), **lists(rng, graph(rng), seeds(rng))}
def setup_inputs_caps(rng):
    o = np.stack([rng.permutation(P) for r in range(N)])
    adj = [[] for a in range(N * P)]
    dense = int(rng.integers(0, N))
    for r in range(N):
        q = (r + 1) % N
        if r == dense:
            a = P * r + np.concatenate([o[r, S:S + K], o[r, K + B:2 * B]])
            c = P * q + np.concatenate([o[q, :S // 2], rng.permutation(np.concatenate([o[q, S // 2:S], o[q, S + K:K + B]]))])
            for i in range(B):
                for j in range(i - i % M, min(i - i % M + M, B)): link(adj, a[i], c[j])
        else:
            for i in range(K):
                link(adj, P * r + o[r, S + i], P * q + o[q, i])
                link(adj, P * r + o[r, S + i], P * q + o[q, S + K + i % (B - S)])
    for r in range(N): inner(rng, adj, P * r + o[r, S:])
    return {**plain(rng), **lists(rng, adj, o[:, :S])}
def setup_inputs_few(rng):
    adj, s, o, n, m = [[] for a in range(N * P)], seeds(rng), rng.permutation(N), K // 2 - 1, S // 2
    some, rest = int(o[1]), sorted(o[2:].tolist())
    ends = np.unique([0, 127, P - 1])
    s[some] = rng.permutation(np.setdiff1d(np.arange(P), ends))[:S]
    free, at, zero = rng.permutation(np.setdiff1d(np.arange(P), np.concatenate([s[some], ends]))), 0, []
    for i in range(K // 2):
        end = s[some, i]
        for t in range(1 + i % R):
            link(adj, P * some + end, P * some + free[at])
            end = free[at]
            at += 1
        if i < K // 4: zero.append(int(end))
    idle = np.sort(free[at:])
    lone = np.concatenate([ends, idle[:n - ends.size]])
    idle = rng.permutation(idle[n - ends.size:])
    for i in range(idle.size): link(adj, P * some + idle[i - 1], P * some + idle[i])
    for r in rest[:2]:
        g, e = rng.permutation(P // 8)[:n], P // 8 + rng.permutation(P // 8)[:m]
        s[r] = rng.permutation(np.setdiff1d(np.arange(P), np.concatenate([g, e])))[:S]
        high = rng.permutation(np.setdiff1d(np.arange(3 * P // 8, P), s[r]))
        for i in range(K): link(adj, P * r + s[r, i], P * r + high[i])
        for i in range(n):
            link(adj, P * r + s[r, i], P * r + g[i])
            link(adj, P * some + lone[i], P * r + g[i])
        for i in range(m):
            link(adj, P * r + s[r, n + i], P * r + e[i])
            link(adj, P * some + s[some, m + i], P * r + e[i])
    across(rng, adj, rest)
    for r in rest: inner(rng, adj, np.arange(P * r, P * r + P))
    sign = np.ones(N)
    sign[rest[::2]] = -0.75
    j = np.arange(P)
    v = f(rng, N, 128, 4 * P).astype(np.float32).reshape(N, 128, P, 4)
    v[:, :64] = 0
    for r in range(N):
        on = np.isin(j, s[r])
        v[r][64:96][:, ~on] = 0
        v[r][96:][:, on] = 0
        v[r, 0, :, 0] = 1024.0 * np.where(on, 1.0, sign[r])
        v[r, 40, :, 0] = np.where(on, rng.integers(1, 3, P), 0.125 * (8 * j // P))
    for r in rest[:2]: v[r, 40, s[r, n:n + m], 0] = 2.0
    v[some, 40, s[some, m:], 0] = 1.0
    v[some, 0, lone, 0] = 4096.0
    v[some][:, zero] = 0
    return {**plain(rng), "x": big(v.reshape(N, 128, 4 * P)), **lists(rng, adj, s)}
def setup_inputs_huge(rng):
    s = seeds(rng)
    v = rng.random((N, 128, P, 4), dtype=np.float32)
    for r in range(N):
        on = np.isin(np.arange(P), s[r])[None, :, None]
        u = ((0.7 + 0.85 * rng.random(P)) * (1 - 2 * (r % 2)))[None, :, None]
        v[r] = np.where(on, 1.7 + 0.28 * v[r], (0.8 + 0.45 * v[r]) * u)
    return {**plain(rng), "x": big((v * np.float32(2.0 ** 29)).reshape(N, 128, 4 * P)), **lists(rng, graph(rng), s)}
def setup_inputs_spread(rng):
    return {**setup_inputs(rng), "x": big(wide(rng, N, 128, 4 * P, cols=6))}
def setup_inputs_ties(rng):
    g = rng.integers(4, 8, (128, 3, 4)) * np.exp2(rng.integers(-2, 1, (128, 3, 4))) * rng.choice([-1.0, 1.0], (128, 3, 4)) * np.exp2(rng.integers(-2, 3, (128, 3, 1)))
    h = rng.integers(0, 3, (N, P))
    h[::2] = 0
    return {**plain(rng), "x": big(np.stack([g[:, h[r]].reshape(128, -1) for r in range(N)])), **lists(rng, graph(rng), seeds(rng), late=True)}
def check_inputs(d):
    b = []
    for k, low in (("x", 2.0 ** -16), ("w", 2.0 ** -30)):
        v = np.abs(d[k].astype(np.float32))
        if not (np.isfinite(v).all() and ((v == 0) | (v >= low) & (v <= 2.0 ** 30)).all()): b.append("a value of " + k)
    for r in range(N):
        e = entries(d["sd"][r])
        if e.min() < 0 or e.max() >= P or np.unique(e).size != S: b.append("sd")
    e = np.concatenate([entries(d["nb"][r]).reshape(M, P) for r in range(N)], axis=1).astype(np.int64)
    if e.min() < -1 or e.max() >= N * P: return b + ["nb"]
    k, j = np.nonzero(e >= 0)
    n = e[k, j]
    a, c = j * (N * P) + n, n * (N * P) + j
    if (n == j).any() or np.unique(a).size != a.size: b.append("nb names a place twice or itself")
    if not np.array_equal(np.sort(a), np.sort(c)): b.append("nb isn't symmetric")
    for r in range(N):
        for q in range(N):
            if q != r and np.count_nonzero((e[:, P * r:P * r + P] // P == q).any(axis=0)) > B: b.append("places with neighbours on one other rank")
    return b
def reference(x, w, nb, sd):
    first = join(*[mx_ref.quantize(np.ascontiguousarray(x[r])) for r in range(N)])
    now = first
    near = np.concatenate([entries(nb[r]).reshape(M, P) for r in range(N)], axis=1)
    parent = np.full(N * P, -1)
    fresh = np.concatenate([P * r + entries(sd[r]) for r in range(N)])
    parent[fresh] = fresh
    score = np.full((M, N * P), -np.inf, np.float32)
    for t in range(R):
        spot = np.full(N * P + 1, -1)
        spot[fresh] = np.arange(fresh.size)
        side = pick(now, np.concatenate([fresh, np.full(4 + -fresh.size % 4, -1)]))
        z = np.concatenate([mx_ref.matmul(pick(first, np.arange(i, i + 128)), side) for i in range(0, N * P, 128)])
        k, j = np.nonzero(spot[near] >= 0)
        score[k, j] = z[j, spot[near[k, j]]] + np.float32(0)
        best, at = score.max(axis=0), score.argmax(axis=0)
        chosen = []
        for r in range(N):
            mine = np.arange(P * r, P * r + P)
            c = mine[(parent[mine] < 0) & np.isfinite(best[mine])]
            chosen.append(c[np.argsort(-best[c], kind="stable")[:K]])
        fresh = np.concatenate(chosen)
        parent[fresh] = near[at[fresh], fresh]
        pad = np.full(4 + -fresh.size % 4, -1)
        v = decode(pick(now, np.concatenate([fresh, pad, parent[fresh], pad])))
        h = v.shape[1] // 2
        new = mx_ref.quantize(np.ascontiguousarray(((v[:, :h] + v[:, h:]) * np.float32(0.5)).astype(BF)))
        now = put(now, fresh, pick(new, np.arange(fresh.size)))
    y, pa = np.zeros((N, 128, O * P), np.float32), np.zeros((N, 1, P), np.float32)
    oc, osc = np.zeros((N, 128, 4 * P), np.uint8), np.zeros((N, 16, P), np.uint8)
    for r in range(N):
        mine = np.arange(P * r, P * r + P)
        q = pick(now, mine)
        for o in range(O): y[r, :, P * o:P * o + P] = mx_ref.matmul(mx_ref.quantize(np.ascontiguousarray(cut(w[r], o))), q)
        oc[r], osc[r] = emit(q)
        pa[r, 0] = parent[mine]
    return {"y": y, "oc": oc, "osc": osc, "pa": pa}

@@ -1,0 +1,445 @@
+from concourse.bass import DstId, RemoteDMATransfer
+from concourse.mybir import dt, AluOpType, ActivationFunctionType
+
+N, P, S, K, R, M, O = 4, 384, 32, 32, 4, 3, 2
+F32, BF, I32, U16, Q4, U8 = "float32", "bfloat16", "int32", "uint16", "float8_e4m3fn_x4", "uint8"
+NG = N * P
+NONE = NG
+SPW = NG + 16
+EMPTY = 2048
+SH = 14
+OLD, NEGC = P, P + 144
+NEG = -1e29
+SEG = 194
+TINY = 2.0 ** -80
+STEP = 2.0 ** -24 * (1 + 2.0 ** -8)
+
+_BUF = {
+    BF: dict(xs=4 * P, ws=512 * O, et=2048, zb=1024, eye=128, fv=64 * R, ma=3 * SEG, mb=3 * SEG, sg=192, rk=3 * SEG,
+             hg=4 * P, hf=4 * 512, bt=4 * 224, fr=2 * EMPTY + 2 * P, ft=2 * P),
+    I32: dict(nbr=72, sdr=8, pi=8, wy=2, wi=2, f1=2, f2=2, f3=2),
+    U16: dict(ids=16 * R, sdl=2, sl=24, gl=2, n9u=16, nbu=12, off=10, wl=4, fo=4, fu=24),
+    Q4: dict(first=P, stat=P, fw=608, fin=P, wq=128 * O, eq=512, new0=224, new1=224, new2=224, new3=224),
+    U8: dict(firsts=P, stats=P, fws=608, fins=P, wqs=128 * O, eqs=512, news0=224, news1=224, news2=224, news3=224),
+    F32: dict(pf=8, i128=128, i16=192, iz=144, dm=192, rs=192, mz=144, tri=32, tri0=32, s2=2, z32=32, slots=64, val=128 * R,
+              ct=36, oldn=9, jj=3, js=3, w16=24, jw=24, slb=24, gl0=5, rs3=9, rs48=144,
+              spot=EMPTY + NG, nbf=72, n9=16, n9a=16, n9b=16, gz=144, nbs=144, nbc=12, dn=9, g2=192, sp=192, fl=9, xx=9, zz=9,
+              oo=9, uu=3, p8=9, dd=9, t2=9, t3=3, cand=3, t4=3, t5=3, zw0=536, zw1=536, gg=144, bb=144, ab=3, hi=6, ne=9,
+              ee=192, rr=480, rk3=3, pp=9, npp=1, ad=64, aa=192, at=192, wp=96, wx=2, pg=9, pas=3, tk=3, tk2=3, pd=3, pd2=3,
+              gb=128, f4=24, ys=O * P),
+}
+SCRATCH = {n: ("sbuf", [128, w], d) for d, b in _BUF.items() for n, w in b.items()}
+SCRATCH["pz"] = ("psum", [128, 512 * 3], F32)
+SCRATCH["pe"] = ("psum", [128, 512 * 4], F32)
+
+SEMAPHORES = ["cv", "cs", "ct", "cg", "sent", "lx", "lw", "lnb", "lsd", "st"] + \
+    ["aid%d" % t for t in range(R)] + ["acol%d" % t for t in range(R)]
+
+A = AluOpType
+AF = ActivationFunctionType
+
+
+def rank_program(g, core, T, topo):
+    rank = T.rank_of(core)
+    if rank is None:
+        return
+    Q = {"v": g.vector, "s": g.scalar, "t": g.tensor, "g": g, "y": g.sync}
+    own = {"v": "cv", "s": "cs", "t": "ct", "g": "cg"}
+    count = {}
+    known = {q: {} for q in Q}
+    log = {}
+
+    def V(name, a=0, b=None, st=1, p=(0, 128)):
+        if b is None:
+            b = SCRATCH[name][1][1]
+        x = T[name][p[0]:p[1], a:b:st] if st != 1 else T[name][p[0]:p[1], a:b]
+        cols = range(a, b, st)
+        if SCRATCH[name][0] == "psum":
+            cols = range(a // 512 * 512, (b + 511) // 512 * 512)
+        return (x, [(name, p, frozenset(cols))])
+
+    def W(name, a, n, p=(0, 128)):
+        return V(name, a, a + n, 1, p)
+
+    def ind(win, offs):
+        return (win[0].indirect(offs[0]), win[1] + offs[1])
+
+    def u8(v):
+        return (v[0].bitcast(dt.uint8), v[1])
+
+    def u32(v):
+        return (v[0].bitcast(dt.uint32), v[1])
+
+    def need(q, ev):
+        sem, val, clock = ev
+        if known[q].get(sem, 0) >= val:
+            return
+        Q[q].wait_ge(T.sem[sem], val)
+        known[q][sem] = val
+        for k2, v2 in clock.items():
+            if known[q].get(k2, 0) < v2:
+                known[q][k2] = v2
+
+    def hazards(reads, writes):
+        best = {}
+        for accs, wr in ((reads, False), (writes, True)):
+            for name, p, cols in accs:
+                ps = SCRATCH[name][0] == "psum"
+                for (p2, c2, w2, ev) in log.get(name, []):
+                    if (wr or w2 or ps) and p[0] < p2[1] and p2[0] < p[1] and not cols.isdisjoint(c2):
+                        if ev[0] not in best or best[ev[0]][1] < ev[1]:
+                            best[ev[0]] = ev
+        return sorted(best.values(), key=lambda e: -sum(e[2].values()))
+
+    def note(reads, writes, ev):
+        for accs, wr in ((reads, False), (writes, True)):
+            for name, p, cols in accs:
+                log.setdefault(name, []).append((p, cols, wr, ev))
+
+    def run(q, fn, outs, ins, sem=None, inc=1):
+        reads, writes = [], []
+        for v in ins:
+            if isinstance(v, tuple):
+                reads += v[1]
+        for v in outs:
+            writes += v[1][:1]
+            reads += v[1][1:]
+        for ev in hazards(reads, writes):
+            need(q, ev)
+        sem = sem or own[q]
+        count[sem] = count.get(sem, 0) + inc
+        fn().then_inc(T.sem[sem], inc)
+        note(reads, writes, (sem, count[sem], dict(known[q])))
+
+    def ap(v):
+        return v[0] if isinstance(v, tuple) else v
+
+    def ts(out, in0, s1, op0, s2=None, op1=None):
+        if op1 is None:
+            run("v", lambda: g.vector.tensor_scalar(out[0], in0[0], ap(s1), None, op0), [out], [in0, s1])
+        else:
+            run("v", lambda: g.vector.tensor_scalar(out[0], in0[0], ap(s1), ap(s2), op0, op1), [out], [in0, s1, s2])
+
+    def tt(out, in0, in1, op):
+        run("v", lambda: g.vector.tensor_tensor(out[0], in0[0], in1[0], op), [out], [in0, in1])
+
+    def cp(out, in_):
+        run("v", lambda: g.vector.tensor_copy(out[0], in_[0]), [out], [in_])
+
+    def ms(out, c):
+        run("v", lambda: g.vector.memset(out[0], c), [out], [])
+
+    def scan(out, d0, d1, op0, op1, init=0.0):
+        run("v", lambda: g.vector.tensor_tensor_scan(out[0], d0[0], d1[0], init, op0, op1), [out], [d0, d1])
+
+    def tr(out, in_):
+        run("v", lambda: g.vector.transpose(out[0], in_[0]), [out], [in_])
+
+    def quant(name, a, n, in_):
+        out, sc = W(name[0], a, n), W(name[1], a, n)
+        run("v", lambda: g.vector.quantize_mx(out[0], sc[0], in_[0]), [out, sc], [in_])
+
+    def act(out, in_, func=AF.Identity, bias=None, scale=None):
+        kw = {}
+        if bias is not None:
+            kw["bias"] = ap(bias)
+        if scale is not None:
+            kw["scale"] = ap(scale)
+        run("s", lambda: g.scalar.activation(out[0], in_[0], func, **kw), [out], [in_, bias, scale])
+
+    def mm(bank, k, lhs, a, rhs, b, n):
+        out, l, ls, r, rs = W(bank, 512 * k, n), W(lhs[0], a, 128), W(lhs[1], a, 128), W(rhs[0], b, n), W(rhs[1], b, n)
+        run("t", lambda: g.tensor.matmul_mx(out[0], l[0], ls[0], r[0], rs[0], True, True), [out], [l, ls, r, rs])
+
+    def iota(out, pattern, base, cm):
+        run("g", lambda: g.iota(out[0], pattern, base, cm, allow_small_or_imprecise_dtypes=True), [out], [])
+
+    def loads(q, sem, pairs):
+        for out, src in pairs:
+            Q[q].dma_start(out[0], src).then_inc(T.sem[sem], 16)
+        count[sem] = 16 * len(pairs)
+        for out, src in pairs:
+            note([], out[1], (sem, count[sem], dict(known[q])))
+
+    def store(q, dst, in_):
+        run(q, lambda: Q[q].dma_start(dst, in_[0]), [], [in_], sem="st", inc=16)
+
+    FIRST, STAT, FW, FIN, WQ, EQ = [(n, n + "s") for n in ("first", "stat", "fw", "fin", "wq", "eq")]
+    NEW = [("new%d" % t, "news%d" % t) for t in range(R)]
+    peers = [(rank + d) % N for d in range(1, N)]
+    mask = -1
+    for q in peers:
+        mask &= topo.mask(core, T.cores[q])
+    neng = bin(mask).count("1")
+    dst_ids = [DstId(rid=topo.addr(T.cores[q])[0], pnc=topo.addr(T.cores[q])[1]) for q in peers]
+
+    def send(name, a, n, sem, cast=None):
+        view = (lambda v: cast(v)) if cast else (lambda v: v)
+        src = view(W(name, a, n))
+        for ev in hazards(src[1], []):
+            need("g", ev)
+        x = RemoteDMATransfer(dst_ids=dst_ids, dma_engine_mask=mask, remote_sem=T.sem[sem], srcs=[src[0]],
+                              dsts=[view(W(name, a + n * ((rank - q) % N), n))[0] for q in peers])
+        g.remote_dma_fused([x], local_sem=T.sem.sent)
+        count["sent"] = count.get("sent", 0) + neng
+
+    def send_ids(t):
+        send("ids", 16 * t + 6, 2, "aid%d" % t)
+
+    def send_cols(t):
+        send(NEW[t][0], 96, 32, "acol%d" % t, u8)
+        send(NEW[t][1], 96, 32, "acol%d" % t)
+
+    for t in range(R):
+        for views, sem, calls in (([W("ids", 16 * t + 8, 6)], "aid%d" % t, 1),
+                                  ([W(NEW[t][0], 128, 96), W(NEW[t][1], 128, 96)], "acol%d" % t, 2)):
+            count[sem] = calls * (N - 1) * neng
+            for v in views:
+                note([], v[1], (sem, count[sem], {}))
+
+    quads = [(32 * a, 32 * a + 32) for a in range(4)]
+    halves = [(0, 64), (64, 128)]
+
+    loads("y", "lx", [(V("xs"), T.x[:])])
+    loads("s", "lsd", [(V("sdr", 0, 2, p=(0, 16)), T.sd[:]), (V("sdr", 0, 2, p=(16, 32)), T.sd[:])])
+    loads("y", "lnb", [(V("nbr", p=(0, 16)), T.nb[:]), (V("nbr", p=(16, 32)), T.nb[:])])
+    need("y", ("acol0", count["acol0"], {}))
+    loads("y", "lw", [(V("ws"), T.w[:])])
+
+    run("g", lambda: g.iota(T.pi[:, 0:1], [[0, 1]], 0, 1), [W("pi", 0, 1)], [])
+    iota(V("i128"), [[1, 128]], 0, 0)
+    iota(V("spot", 0, SPW // 2), [[-1, SPW // 2]], -1, 0)
+    iota(V("i16"), [[0, 12], [1, 16]], 0, 0)
+    ms(V("zb"), 0.0)
+    act(W("et", 0, 1024), V("zb"))
+    act(W("et", 1024, 1024), V("zb"))
+    p0 = W("pi", 0, 1)
+    ts(W("pi", 1, 1), p0, 15, A.bitwise_and)
+    ts(W("pi", 2, 1), p0, 4, A.logical_shift_right)
+    ts(W("pi", 3, 1), p0, 31, A.bitwise_and)
+    ts(W("pi", 4, 1), p0, 5, A.logical_shift_right, 1, A.bitwise_and)
+    ts(W("pi", 5, 1), p0, 6, A.logical_shift_right)
+    ms(V("zw0", OLD, 536), NEG)
+    cp(W("pf", 0, 6), W("pi", 0, 6))
+    pf, r16, grp, u32c, odd, upper = [W("pf", i, 1) for i in range(6)]
+    ms(V("zw1", NEGC, 536), NEG)
+    ms(V("rs3"), 0.0)
+    ms(V("rs48"), 0.0)
+    ts(V("eye"), V("i128"), pf, A.is_equal)
+    ts(W("gl0", 4, 1), r16, 3.0, A.mult)
+    ts(W("gl0", 1, 1), r16, 3.0, A.is_ge, 21.0, A.mult)
+    ts(W("gl0", 2, 1), r16, 6.0, A.is_ge, 21.0, A.mult)
+    ts(W("gl0", 3, 1), grp, 3.0, A.mult, r16, A.add)
+    ts(V("tri0"), W("i128", 0, 32), u32c, A.is_gt, odd, A.subtract)
+    ts(V("s2"), W("pf", 4, 2), -STEP, A.mult, STEP, A.add)
+    ts(W("gl0", 0, 1), W("gl0", 1, 1), W("gl0", 2, 1), A.add, W("gl0", 3, 1), A.add)
+    ts(V("tri"), V("tri0"), STEP, A.mult)
+    ms(V("ne"), 0.0)
+    ts(W("gl", 0, 1), W("gl0", 0, 1), 71.0, A.min)
+    ms(V("z32"), 0.0)
+    ms(V("rs3", 0, 9, 3), 9 * NEG)
+    ms(V("rs48", 0, 144, 48), 9 * NEG)
+    for c in range(2):
+        ms(V("ma", 192 + c, 3 * SEG, SEG), 0.0)
+        ms(V("mb", 192 + c, 3 * SEG, SEG), 0.0)
+    for a in quads:
+        cp(V("sdl", p=a), W("sdr", 0, 2, (0, 32)))
+    ts(W("ids", 6, 2), V("sdl"), float(P * rank), A.add)
+    act(V("spot", SPW // 2, SPW), V("spot", 0, SPW // 2), bias=float(-(SPW // 2)))
+    send_ids(0)
+    iota(V("iz"), [[0, 3], [1, 16], [0, 3]], 0, 0)
+    iota(V("slb"), [[1, 3], [48, 8]], 0, 0)
+    iota(V("jj"), [[1, 3]], P * rank, 3)
+    for b in range(4):
+        act(V("et", 512 * b + b, 512 * b + 512, 4), V("eye"))
+    for a in quads:
+        cp(V("nbf", p=a), V("nbr", p=(0, 32)))
+    cp(V("n9"), ind(V("nbf"), W("gl", 0, 1)))
+    ts(V("dm"), V("i16"), r16, A.not_equal, 2 * NEG, A.mult)
+    ts(V("n9a"), V("n9"), 0.0, A.is_lt, float(NONE + 1), A.mult)
+    quant(FIRST, 0, P, V("xs"))
+    cp(u32(W("new0", 96, 32)), ind(u32(V("first")), V("sdl")))
+    act(W("news0", 96, 32), ind(V("firsts"), V("sdl")), AF.Copy)
+    send_cols(0)
+    iota(V("ct"), [[-128, 4], [80, 3], [-16, 3]], -(OLD + 15), 0)
+    iota(V("oldn"), [[48, 3], [16, 3]], OLD + 15 - NEGC, 0)
+    iota(V("js"), [[1 << SH, 3]], 0, 3 << SH)
+    iota(V("slots"), [[16, 2], [0, 2], [1, 16]], 0, 0)
+    iota(V("bt"), [[0, 4 * 224]], 0, 0)
+    iota(V("w16"), [[16, 24]], -(P - 1), 0)
+    iota(V("fv"), [[32, 4], [0, 2], [1, 32]], 1, 0)
+    iota(V("val", 128, 128 * R), [[1, 128 * (R - 1)]], 128, 0)
+    ts(V("sl"), V("slb"), W("gl0", 4, 1), A.add)
+    tt(V("n9b"), V("n9a"), V("n9"), A.add)
+    quant(EQ, 0, 512, V("et"))
+    for b in range(4):
+        mm("pe", b, EQ, 128 * b, FIRST, 0, P)
+    act(V("stats"), ind(V("firsts"), V("sl")), AF.Copy)
+    for b in range(4):
+        act(W("hg", P * b, P), W("pe", 512 * b, P), scale=0.5)
+    cp(V("n9u"), V("n9b"))
+    ts(V("mz"), V("iz"), r16, A.not_equal, 2 * NEG, A.mult)
+    ts(V("rs"), V("i16"), 0.0, A.is_equal, 9 * NEG, A.mult)
+    tt(V("gz"), ind(V("spot", 0, SPW), W("n9u", 0, 9)), V("mz"), A.add)
+    cp(W("nbc", 9, 3), V("jj"))
+    for c in range(3):
+        scan(W("nbs", 48 * c, 48), W("rs", 0, 48), V("gz", c, 144, 3), A.add, A.max)
+    for k in range(M):
+        ts(V("nbc", 2 - k, 9, 3), V("nbs", 16 * k + 15, 144, 48), -1.0, A.mult, -1.0, A.add)
+
+    def later(t):
+        if t == 0:
+            ms(V("fr", 0, 2 * P), -1024.0)
+            tt(V("dn", 0, 9, 3), V("nbc", 0, 9, 3), V("nbc", 1, 9, 3), A.subtract)
+            tt(V("dn", 1, 9, 3), V("nbc", 1, 9, 3), V("nbc", 2, 9, 3), A.subtract)
+            cp(V("dn", 2, 9, 3), V("nbc", 2, 9, 3))
+            ts(V("pd"), V("jj"), 1.0, A.add)
+            tt(V("pd2"), V("pd"), V("uu"), A.mult)
+            tt(V("pas"), V("jj"), V("pd2"), A.subtract)
+        if t == 1:
+            quant(FW, 0, P, V("xs"))
+        if t == 2:
+            quant(WQ, 0, 128 * O, V("ws"))
+            ts(V("jw"), V("w16"), r16, A.add)
+
+    def parents():
+        scan(V("pg"), V("ne"), V("dn"), A.mult, A.add)
+        ts(V("tk"), V("rk3"), float(K), A.is_lt)
+        tt(V("pd"), V("pg", 2, 9, 3), V("pas"), A.subtract)
+        tt(V("tk2"), V("tk"), V("cand"), A.mult)
+        tt(V("pd2"), V("pd"), V("tk2"), A.mult)
+        tt(V("pas"), V("pas"), V("pd2"), A.add)
+
+    def mark_offsets():
+        ts(V("f1"), V("wy"), SH, A.logical_shift_right, 15, A.bitwise_and)
+        ts(V("f2"), V("wy"), SH - 1, A.logical_shift_right)
+        tt(V("f3"), V("f2"), V("f1"), A.subtract)
+        for d in range(2):
+            ts(W("fo", 2 * d, 2), V("f3"), float(16 * d), A.add)
+
+    def mark(t):
+        cp(ind(V("fr"), V("fo")), W("fv", 64 * t, 64))
+
+    for t in range(R):
+        zw, zn, last = "zw%d" % (t % 2), "zw%d" % ((t + 1) % 2), t == R - 1
+        cp(ind(V("spot"), W("ids", 16 * t + 6, 8)), V("i128") if t == 0 else W("val", 128 * t, 128))
+        if t == 0:
+            cp(V("nbu"), V("nbc"))
+            cp(u32(V("stat")), ind(u32(V("first")), V("sl")))
+        tt(V("g2"), ind(V("spot", 0, SPW), V("nbu")), V("dm"), A.add)
+        scan(V("sp"), V("rs"), V("g2"), A.add, A.max)
+        sp9 = V("sp", 15, 144, 16)
+        ts(V("fl"), sp9, float(128 * t), A.is_ge)
+        tt(V("xx"), sp9, W("ct", 9 * t, 9), A.add)
+        ts(V("uu"), V("sp", 159, 192, 16), 0.0, A.is_lt)
+        tt(V("zz"), V("xx"), V("fl"), A.mult)
+        scan(V("t2"), V("rs3"), sp9, A.add, A.max)
+        tt(V("oo"), V("zz"), V("oldn"), A.add)
+        ts(V("t3"), V("t2", 2, 9, 3), 0.0, A.is_ge)
+        for c in range(3):
+            ts(W("off", 3 * c, 3), W("oo", 3 * c, 3), W("uu", c, 1), A.mult, float(NEGC), A.add)
+        for c in range(3):
+            ts(W("p8", 3 * c, 3), V("sp", 48 * c + 15, 48 * c + 48, 16), 0.0, A.max, W("uu", c, 1), A.mult)
+        tt(V("cand"), V("t3"), V("uu"), A.mult)
+        tt(V("t4"), V("p8", 2, 9, 3), V("js"), A.add)
+        ts(V("t5"), V("cand"), -float(EMPTY << SH), A.mult, float(EMPTY << SH), A.add)
+        tt(V("dd", 0, 9, 3), V("p8", 0, 9, 3), V("p8", 1, 9, 3), A.subtract)
+        tt(V("dd", 1, 9, 3), V("p8", 1, 9, 3), V("p8", 2, 9, 3), A.subtract)
+        tt(V("dd", 2, 9, 3), V("t4"), V("t5"), A.add)
+        for c in range(3):
+            mm("pz", c, STAT, 128 * c, NEW[t], 96, 128)
+        for b in range(4):
+            mm("pe", b, EQ, 128 * b, NEW[t], 96, 128)
+        act(W(zw, 0, 128), W("pz", 0, 128), bias=TINY)
+        ts(W(zw, 128, 128), W("pz", 512, 128), TINY, A.add)
+        act(W(zw, 256, 128), W("pz", 1024, 128), bias=TINY)
+        tt(V("gg"), ind(V(zw), W("off", 0, 9)), W("dm", 0, 144), A.add)
+        scan(V("bb"), V("rs48"), V("gg"), A.add, A.max)
+        vc = [W("bb", 48 * c + 47, 1) for c in range(3)]
+        act(V("ab"), V("bb", 47, 144, 48), AF.Abs)
+        for c in range(3):
+            act(W("ee", 32 * c, 32), V("z32"), bias=vc[c])
+        scan(W(zn, OLD, 144), W("rs", 0, 144), V("gg"), A.add, A.max)
+        for c in range(3):
+            ts(W("ee", 96 + 32 * c, 32), V("tri"), W("ab", c, 1), A.mult, vc[c], A.add)
+        for c in range(3):
+            act(W("hi", 2 * c, 2), V("s2"), bias=vc[c], scale=W("ab", c, 1))
+        tr(W("rr", 0, 192), V("ee"))
+        cp(W("rr", 192, 96, quads[0]), W("rr", 0, 96, quads[1]))
+        act(W("rr", 192, 96, quads[2]), W("rr", 0, 96, quads[3]))
+        cp(W("rr", 192, 96, quads[1]), W("rr", 0, 96, quads[0]))
+        act(W("rr", 192, 96, quads[3]), W("rr", 0, 96, quads[2]))
+        for h in range(2):
+            act(W("rr", 288, 96, halves[h]), W("rr", 0, 96, halves[1 - h]))
+        for h in range(2):
+            act(W("rr", 384, 96, halves[h]), W("rr", 192, 96, halves[1 - h]))
+        act(V("sg"), W("rr", 288, 192), AF.Sign, bias=W("hi", 5, 1), scale=-1.0)
+        act(W("mb", 2 * SEG, 192), V("sg"), AF.Relu)
+        for c in range(3):
+            act(W("ne", 3 * c + 1, 2), V(zn, OLD + 48 * c + 31, OLD + 48 * c + 48, 16), AF.Sign, bias=vc[c], scale=-1.0)
+        ts(W("ma", SEG + 192, 1), vc[0], vc[1], A.is_equal)
+        for c in range(3):
+            ts(W("ma", SEG * c, 192), W("rr", 96, 192), W("hi", 2 * c, 1), A.is_ge)
+        ts(W("ma", 2 * SEG + 192, 2), V("bb", 47, 96, 48), vc[2], A.is_equal)
+        for c in range(2):
+            ts(W("mb", SEG * c, 192), W("rr", 288, 192), W("hi", 2 * c + 1, 1), A.is_ge)
+        for c in range(3):
+            scan(W("rk", SEG * c, SEG), W("ma", SEG * c, SEG), W("mb", SEG * c, SEG),
+                 A.add, A.add if c < 2 else A.subtract, 0.0 if c < 2 else 192.0)
+        scan(V("pp"), V("ne"), V("dd"), A.mult, A.add)
+        cp(V("rk3"), V("rk", SEG - 1, 3 * SEG, SEG))
+        act(W("hf", 128 * t, 128), W("pe", 0, 128), scale=0.5)
+        act(V("npp"), W("pp", 8, 1), scale=-1.0)
+        act(V("ad"), V("slots"), AF.Abs, bias=W("rk3", 2, 1), scale=-1.0)
+        for m in range(2):
+            act(W("aa", 96 * m + 64, 32), W("ad", 32 * m, 32), AF.Relu, bias=W("pp", 8, 1), scale=V("npp"))
+        for b in range(1, 4):
+            act(W("hf", 512 * b + 128 * t, 128), W("pe", 512 * b, 128), scale=0.5)
+        for c in range(2):
+            for m in range(2):
+                ts(W("aa", 96 * m + 32 * c, 32), W("slots", 32 * m, 32), W("rk3", c, 1), A.is_equal, W("pp", 3 * c + 2, 1), A.mult)
+        tr(V("at"), V("aa"))
+        for m in range(2):
+            scan(W("wp", 48 * m, 48), W("at", 96 * m, 48), W("at", 96 * m + 48, 48), A.add, A.add)
+        tt(V("wx", p=halves[0]), V("wp", 47, 96, 48, p=halves[0]), V("wp", 47, 96, 48, p=halves[1]), A.add)
+        for a in quads:
+            tt(V("wy", p=a), V("wx", p=quads[0]), V("wx", p=quads[1]), A.add)
+        ts(W("wl", 0, 2), V("wy"), 2.0 ** -SH, A.mult, float(P - 1), A.min)
+        ts(V("wi"), V("wy"), 511, A.bitwise_and)
+        for b in range(4):
+            act(W("gb", 32 * b, 32), ind(W("hg", P * b, P), W("wl", 0, 2)))
+        if not last:
+            ts(W("ids", 16 * t + 22, 2), V("wy"), 2.0 ** -SH, A.mult, float(P * rank), A.add)
+            send_ids(t + 1)
+        cp(W("wl", 2, 2), V("wi"))
+        if last:
+            mark_offsets()
+        for b in range(4):
+            tt(V("bt", 384 + b, 512, 4), ind(W("hf", 512 * b, 128 * t + 128), W("wl", 2, 2)), W("gb", 32 * b, 32), A.add)
+        if not last:
+            quant(NEW[t + 1], 0, 128, W("bt", 0, 512))
+            send_cols(t + 1)
+            later(t)
+            mark_offsets()
+            parents()
+        mark(t)
+        quant(FW, P + 32 * t, 128, W("bt", 384, 512))
+
+    tr(V("ft"), W("fr", 0, 2 * P))
+    tt(V("f4"), V("ft", 0, 2 * P, 32), V("jw"), A.max)
+    ts(V("fu"), V("f4"), float(P - 1), A.add)
+    cp(u32(V("fin")), ind(u32(V("fw")), V("fu")))
+    act(V("fins"), ind(V("fws"), V("fu")), AF.Copy)
+    for o in range(O):
+        mm("pz", o, WQ, 128 * o, FIN, 0, P)
+    parents()
+    store("y", T.oc[:], u8(V("fin")))
+    for k in range(4):
+        store("y", T.osc[4 * k:4 * k + 4, :], V("fins", p=(32 * k, 32 * k + 4)))
+    act(W("ys", 0, P), W("pz", 0, P))
+    store("s", T.y[:, 0:P], W("ys", 0, P))
+    cp(W("ys", P, P), W("pz", 512, P))
+    store("y", T.pa[:], V("pas"))
+    store("y", T.y[:, P:2 * P], W("ys", P, P))
+    for sem, val in count.items():
+        g.wait_ge(T.sem[sem], val)

@@ -22,9 +22,9 @@ _BUF = {
     Q4: dict(first=P, stat=P, fw=608, fin=P, wq=128 * O, eq=512, new0=224, new1=224, new2=224, new3=224),
     U8: dict(firsts=P, stats=P, fws=608, fins=P, wqs=128 * O, eqs=512, news0=224, news1=224, news2=224, news3=224),
     F32: dict(pf=8, i128=128, i16=192, iz=144, dm=192, rs=192, mz=144, tri=32, tri0=32, s2=2, z32=32, slots=64, val=128 * R,
-              ct=36, oldn=9, jj=3, js=3, w16=24, jw=24, slb=24, gl0=5, rs3=9, rs48=144,
-              spot=EMPTY + NG, nbf=72, n9=16, n9a=16, n9b=16, gz=144, nbs=144, nbc=12, dn=9, g2=192, sp=192, fl=9, xx=9, zz=9,
-              oo=9, uu=3, p8=9, dd=9, t2=9, t3=3, cand=3, t4=3, t5=3, zw0=536, zw1=536, gg=144, bb=144, ab=3, hi=6, ne=9,
+              ct=36, jj=3, js=3, w16=24, jw=24, slb=24, gl0=5, rs3=9, rs48=144,
+              spot=EMPTY + NG, nbf=72, n9=16, n9a=16, n9b=16, gz=144, nbs=144, nbc=12, dn=9, g2=192, sp=192, fl=18, xx=18,
+              oo=18, uu=3, p8=9, dd=9, t2=9, t3=3, cand=3, t4=3, t5=3, zw0=536, zw1=536, gg=144, bb=144, ab=3, hi=6, ne=9,
               ee=192, rr=480, rk3=3, pp=9, npp=1, ad=64, aa=192, at=192, wp=96, wx=2, pg=9, pas=3, tk=3, tk2=3, pd=3, pd2=3,
               gb=128, f4=24, ys=O * P),
 }
@@ -239,6 +239,7 @@ def rank_program(g, core, T, topo):
     ms(V("z32"), 0.0)
     ms(V("rs3", 0, 9, 3), 9 * NEG)
     ms(V("rs48", 0, 144, 48), 9 * NEG)
+    ms(V("fl", 0, 18, 2), 0.0)
     for c in range(2):
         ms(V("ma", 192 + c, 3 * SEG, SEG), 0.0)
         ms(V("mb", 192 + c, 3 * SEG, SEG), 0.0)
@@ -262,39 +263,41 @@ def rank_program(g, core, T, topo):
     act(W("news0", 96, 32), ind(V("firsts"), V("sdl")), AF.Copy)
     send_cols(0)
     iota(V("ct"), [[-128, 4], [80, 3], [-16, 3]], -(OLD + 15), 0)
-    iota(V("oldn"), [[48, 3], [16, 3]], OLD + 15 - NEGC, 0)
+    iota(V("xx", 1, 18, 2), [[48, 3], [16, 3]], OLD + 15 - NEGC, 0)
     iota(V("js"), [[1 << SH, 3]], 0, 3 << SH)
     iota(V("slots"), [[16, 2], [0, 2], [1, 16]], 0, 0)
     iota(V("bt"), [[0, 4 * 224]], 0, 0)
     iota(V("w16"), [[16, 24]], -(P - 1), 0)
     iota(V("fv"), [[32, 4], [0, 2], [1, 32]], 1, 0)
     iota(V("val", 128, 128 * R), [[1, 128 * (R - 1)]], 128, 0)
-    ts(V("sl"), V("slb"), W("gl0", 4, 1), A.add)
     tt(V("n9b"), V("n9a"), V("n9"), A.add)
+    ts(V("sl"), V("slb"), W("gl0", 4, 1), A.add)
+    ts(V("mz"), V("iz"), r16, A.not_equal, 2 * NEG, A.mult)
+    cp(V("n9u"), V("n9b"))
     quant(EQ, 0, 512, V("et"))
     for b in range(4):
         mm("pe", b, EQ, 128 * b, FIRST, 0, P)
     act(V("stats"), ind(V("firsts"), V("sl")), AF.Copy)
     for b in range(4):
         act(W("hg", P * b, P), W("pe", 512 * b, P), scale=0.5)
-    cp(V("n9u"), V("n9b"))
-    ts(V("mz"), V("iz"), r16, A.not_equal, 2 * NEG, A.mult)
-    ts(V("rs"), V("i16"), 0.0, A.is_equal, 9 * NEG, A.mult)
     tt(V("gz"), ind(V("spot", 0, SPW), W("n9u", 0, 9)), V("mz"), A.add)
-    cp(W("nbc", 9, 3), V("jj"))
+    ts(V("rs"), V("i16"), 0.0, A.is_equal, 9 * NEG, A.mult)
+    cp(ind(V("spot"), W("ids", 6, 8)), V("i128"))
     for c in range(3):
         scan(W("nbs", 48 * c, 48), W("rs", 0, 48), V("gz", c, 144, 3), A.add, A.max)
+    cp(W("nbu", 9, 3), V("jj"))
     for k in range(M):
-        ts(V("nbc", 2 - k, 9, 3), V("nbs", 16 * k + 15, 144, 48), -1.0, A.mult, -1.0, A.add)
+        ts(V("nbu", 2 - k, 9, 3), V("nbs", 16 * k + 15, 144, 48), -1.0, A.mult, -1.0, A.add)
+    cp(u32(V("stat")), ind(u32(V("first")), V("sl")))
 
     def later(t):
         if t == 0:
-            ms(V("fr", 0, 2 * P), -1024.0)
-            tt(V("dn", 0, 9, 3), V("nbc", 0, 9, 3), V("nbc", 1, 9, 3), A.subtract)
-            tt(V("dn", 1, 9, 3), V("nbc", 1, 9, 3), V("nbc", 2, 9, 3), A.subtract)
-            cp(V("dn", 2, 9, 3), V("nbc", 2, 9, 3))
+            cp(V("nbc"), V("nbu"))
             ts(V("pd"), V("jj"), 1.0, A.add)
+            ms(V("fr", 0, 2 * P), -1024.0)
+            tt(W("dn", 0, 8), W("nbc", 0, 8), W("nbc", 1, 8), A.subtract)
             tt(V("pd2"), V("pd"), V("uu"), A.mult)
+            ts(V("dn", 2, 9, 3), V("nbc", 2, 9, 3), 1.0, A.add)
             tt(V("pas"), V("jj"), V("pd2"), A.subtract)
         if t == 1:
             quant(FW, 0, P, V("xs"))
@@ -303,49 +306,32 @@ def rank_program(g, core, T, topo):
             ts(V("jw"), V("w16"), r16, A.add)
 
     def parents():
-        scan(V("pg"), V("ne"), V("dn"), A.mult, A.add)
-        ts(V("tk"), V("rk3"), float(K), A.is_lt)
-        tt(V("pd"), V("pg", 2, 9, 3), V("pas"), A.subtract)
-        tt(V("tk2"), V("tk"), V("cand"), A.mult)
-        tt(V("pd2"), V("pd"), V("tk2"), A.mult)
-        tt(V("pas"), V("pas"), V("pd2"), A.add)
-
-    def mark_offsets():
-        ts(V("f1"), V("wy"), SH, A.logical_shift_right, 15, A.bitwise_and)
-        ts(V("f2"), V("wy"), SH - 1, A.logical_shift_right)
-        tt(V("f3"), V("f2"), V("f1"), A.subtract)
-        for d in range(2):
-            ts(W("fo", 2 * d, 2), V("f3"), float(16 * d), A.add)
+        for c in range(3):
+            act(W("pas", c, 1), W("pg", 3 * c + 2, 1), bias=W("pas", c, 1), scale=W("tk2", c, 1))
 
     def mark(t):
         cp(ind(V("fr"), V("fo")), W("fv", 64 * t, 64))
 
     for t in range(R):
         zw, zn, last = "zw%d" % (t % 2), "zw%d" % ((t + 1) % 2), t == R - 1
-        cp(ind(V("spot"), W("ids", 16 * t + 6, 8)), V("i128") if t == 0 else W("val", 128 * t, 128))
-        if t == 0:
-            cp(V("nbu"), V("nbc"))
-            cp(u32(V("stat")), ind(u32(V("first")), V("sl")))
-        tt(V("g2"), ind(V("spot", 0, SPW), V("nbu")), V("dm"), A.add)
-        scan(V("sp"), V("rs"), V("g2"), A.add, A.max)
+        n = 12 if t == 0 else 9
+        if t > 0:
+            cp(ind(V("spot"), W("ids", 16 * t + 6, 8)), W("val", 128 * t, 128))
+        tt(W("g2", 0, 16 * n), ind(V("spot", 0, SPW), W("nbu", 0, n)), W("dm", 0, 16 * n), A.add)
+        scan(W("sp", 0, 16 * n), W("rs", 0, 16 * n), W("g2", 0, 16 * n), A.add, A.max)
         sp9 = V("sp", 15, 144, 16)
-        ts(V("fl"), sp9, float(128 * t), A.is_ge)
-        tt(V("xx"), sp9, W("ct", 9 * t, 9), A.add)
-        ts(V("uu"), V("sp", 159, 192, 16), 0.0, A.is_lt)
-        tt(V("zz"), V("xx"), V("fl"), A.mult)
+        ts(V("fl", 1, 18, 2), sp9, float(128 * t), A.is_ge)
+        tt(V("xx", 0, 18, 2), sp9, W("ct", 9 * t, 9), A.add)
+        if t == 0:
+            ts(V("uu"), V("sp", 159, 192, 16), 0.0, A.is_lt)
         scan(V("t2"), V("rs3"), sp9, A.add, A.max)
-        tt(V("oo"), V("zz"), V("oldn"), A.add)
+        scan(V("oo"), V("fl"), V("xx"), A.mult, A.add)
         ts(V("t3"), V("t2", 2, 9, 3), 0.0, A.is_ge)
         for c in range(3):
-            ts(W("off", 3 * c, 3), W("oo", 3 * c, 3), W("uu", c, 1), A.mult, float(NEGC), A.add)
+            ts(W("off", 3 * c, 3), V("oo", 6 * c + 1, 6 * c + 6, 2), W("uu", c, 1), A.mult, float(NEGC), A.add)
         for c in range(3):
-            ts(W("p8", 3 * c, 3), V("sp", 48 * c + 15, 48 * c + 48, 16), 0.0, A.max, W("uu", c, 1), A.mult)
+            act(W("p8", 3 * c, 3), V("sp", 48 * c + 15, 48 * c + 48, 16), AF.Relu, scale=W("uu", c, 1))
         tt(V("cand"), V("t3"), V("uu"), A.mult)
-        tt(V("t4"), V("p8", 2, 9, 3), V("js"), A.add)
-        ts(V("t5"), V("cand"), -float(EMPTY << SH), A.mult, float(EMPTY << SH), A.add)
-        tt(V("dd", 0, 9, 3), V("p8", 0, 9, 3), V("p8", 1, 9, 3), A.subtract)
-        tt(V("dd", 1, 9, 3), V("p8", 1, 9, 3), V("p8", 2, 9, 3), A.subtract)
-        tt(V("dd", 2, 9, 3), V("t4"), V("t5"), A.add)
         for c in range(3):
             mm("pz", c, STAT, 128 * c, NEW[t], 96, 128)
         for b in range(4):
@@ -353,7 +339,9 @@ def rank_program(g, core, T, topo):
         act(W(zw, 0, 128), W("pz", 0, 128), bias=TINY)
         ts(W(zw, 128, 128), W("pz", 512, 128), TINY, A.add)
         act(W(zw, 256, 128), W("pz", 1024, 128), bias=TINY)
+        tt(V("t4"), V("p8", 2, 9, 3), V("js"), A.add)
         tt(V("gg"), ind(V(zw), W("off", 0, 9)), W("dm", 0, 144), A.add)
+        ts(V("t5"), V("cand"), -float(EMPTY << SH), A.mult, float(EMPTY << SH), A.add)
         scan(V("bb"), V("rs48"), V("gg"), A.add, A.max)
         vc = [W("bb", 48 * c + 47, 1) for c in range(3)]
         act(V("ab"), V("bb", 47, 144, 48), AF.Abs)
@@ -364,7 +352,9 @@ def rank_program(g, core, T, topo):
             ts(W("ee", 96 + 32 * c, 32), V("tri"), W("ab", c, 1), A.mult, vc[c], A.add)
         for c in range(3):
             act(W("hi", 2 * c, 2), V("s2"), bias=vc[c], scale=W("ab", c, 1))
+        tt(W("dd", 0, 8), W("p8", 0, 8), W("p8", 1, 8), A.subtract)
         tr(W("rr", 0, 192), V("ee"))
+        ts(W("ma", SEG + 192, 1), vc[0], vc[1], A.is_equal)
         cp(W("rr", 192, 96, quads[0]), W("rr", 0, 96, quads[1]))
         act(W("rr", 192, 96, quads[2]), W("rr", 0, 96, quads[3]))
         cp(W("rr", 192, 96, quads[1]), W("rr", 0, 96, quads[0]))
@@ -374,10 +364,11 @@ def rank_program(g, core, T, topo):
         for h in range(2):
             act(W("rr", 384, 96, halves[h]), W("rr", 192, 96, halves[1 - h]))
         act(V("sg"), W("rr", 288, 192), AF.Sign, bias=W("hi", 5, 1), scale=-1.0)
+        act(W("ne", 1, 2), V(zn, OLD + 31, OLD + 48, 16), AF.Sign, bias=vc[0], scale=-1.0)
         act(W("mb", 2 * SEG, 192), V("sg"), AF.Relu)
-        for c in range(3):
+        for c in range(1, 3):
             act(W("ne", 3 * c + 1, 2), V(zn, OLD + 48 * c + 31, OLD + 48 * c + 48, 16), AF.Sign, bias=vc[c], scale=-1.0)
-        ts(W("ma", SEG + 192, 1), vc[0], vc[1], A.is_equal)
+        tt(V("dd", 2, 9, 3), V("t4"), V("t5"), A.add)
         for c in range(3):
             ts(W("ma", SEG * c, 192), W("rr", 96, 192), W("hi", 2 * c, 1), A.is_ge)
         ts(W("ma", 2 * SEG + 192, 2), V("bb", 47, 96, 48), vc[2], A.is_equal)
@@ -390,7 +381,7 @@ def rank_program(g, core, T, topo):
         cp(V("rk3"), V("rk", SEG - 1, 3 * SEG, SEG))
         act(W("hf", 128 * t, 128), W("pe", 0, 128), scale=0.5)
         act(V("npp"), W("pp", 8, 1), scale=-1.0)
-        act(V("ad"), V("slots"), AF.Abs, bias=W("rk3", 2, 1), scale=-1.0)
+        act(V("ad"), V("slots"), AF.Abs, bias=W("rk", 3 * SEG - 1, 1), scale=-1.0)
         for m in range(2):
             act(W("aa", 96 * m + 64, 32), W("ad", 32 * m, 32), AF.Relu, bias=W("pp", 8, 1), scale=V("npp"))
         for b in range(1, 4):
@@ -398,33 +389,41 @@ def rank_program(g, core, T, topo):
         for c in range(2):
             for m in range(2):
                 ts(W("aa", 96 * m + 32 * c, 32), W("slots", 32 * m, 32), W("rk3", c, 1), A.is_equal, W("pp", 3 * c + 2, 1), A.mult)
+        ts(V("tk"), V("rk3"), float(K), A.is_lt)
         tr(V("at"), V("aa"))
+        tt(V("tk2"), V("tk"), V("cand"), A.mult)
         for m in range(2):
             scan(W("wp", 48 * m, 48), W("at", 96 * m, 48), W("at", 96 * m + 48, 48), A.add, A.add)
         tt(V("wx", p=halves[0]), V("wp", 47, 96, 48, p=halves[0]), V("wp", 47, 96, 48, p=halves[1]), A.add)
         for a in quads:
             tt(V("wy", p=a), V("wx", p=quads[0]), V("wx", p=quads[1]), A.add)
         ts(W("wl", 0, 2), V("wy"), 2.0 ** -SH, A.mult, float(P - 1), A.min)
-        ts(V("wi"), V("wy"), 511, A.bitwise_and)
-        for b in range(4):
-            act(W("gb", 32 * b, 32), ind(W("hg", P * b, P), W("wl", 0, 2)))
         if not last:
             ts(W("ids", 16 * t + 22, 2), V("wy"), 2.0 ** -SH, A.mult, float(P * rank), A.add)
             send_ids(t + 1)
+        ts(V("wi"), V("wy"), 511, A.bitwise_and)
+        for b in range(4):
+            act(W("gb", 32 * b, 32), ind(W("hg", P * b, P), W("wl", 0, 2)))
+        ts(V("f1"), V("wy"), SH, A.logical_shift_right, 15, A.bitwise_and)
         cp(W("wl", 2, 2), V("wi"))
-        if last:
-            mark_offsets()
+        ts(V("f2"), V("wy"), SH - 1, A.logical_shift_right)
         for b in range(4):
             tt(V("bt", 384 + b, 512, 4), ind(W("hf", 512 * b, 128 * t + 128), W("wl", 2, 2)), W("gb", 32 * b, 32), A.add)
         if not last:
             quant(NEW[t + 1], 0, 128, W("bt", 0, 512))
             send_cols(t + 1)
             later(t)
-            mark_offsets()
-            parents()
-        mark(t)
+        tt(V("f3"), V("f2"), V("f1"), A.subtract)
+        scan(V("pg"), V("ne"), V("dn"), A.mult, A.add)
+        for d in range(2):
+            ts(W("fo", 2 * d, 2), V("f3"), float(16 * d), A.add)
+        parents()
         quant(FW, P + 32 * t, 128, W("bt", 384, 512))
+        mark(t)
+        if not last:
+            tt(V("uu"), V("uu"), V("tk2"), A.subtract)
 
+    store("y", T.pa[:], V("pas"))
     tr(V("ft"), W("fr", 0, 2 * P))
     tt(V("f4"), V("ft", 0, 2 * P, 32), V("jw"), A.max)
     ts(V("fu"), V("f4"), float(P - 1), A.add)
@@ -432,14 +431,12 @@ def rank_program(g, core, T, topo):
     act(V("fins"), ind(V("fws"), V("fu")), AF.Copy)
     for o in range(O):
         mm("pz", o, WQ, 128 * o, FIN, 0, P)
-    parents()
     store("y", T.oc[:], u8(V("fin")))
     for k in range(4):
         store("y", T.osc[4 * k:4 * k + 4, :], V("fins", p=(32 * k, 32 * k + 4)))
     act(W("ys", 0, P), W("pz", 0, P))
     store("s", T.y[:, 0:P], W("ys", 0, P))
     cp(W("ys", P, P), W("pz", 512, P))
-    store("y", T.pa[:], V("pas"))
     store("y", T.y[:, P:2 * P], W("ys", P, P))
     for sem, val in count.items():
         g.wait_ge(T.sem[sem], val)

@@ -8,28 +8,30 @@ NONE = NG
 SPW = NG + 16
 EMPTY = 2048
 SH = 14
-OLD, NEGC = P, P + 144
+POS = 8
+WIN = 528
 NEG = -1e29
 SEG = 194
 TINY = 2.0 ** -80
 STEP = 2.0 ** -24 * (1 + 2.0 ** -8)
+MID = 208
 
 _BUF = {
-    BF: dict(xs=4 * P, ws=512 * O, et=2048, zb=1024, eye=128, fv=64 * R, ma=3 * SEG, mb=3 * SEG, sg=192, rk=3 * SEG,
-             hg=4 * P, hf=4 * 512, bt=4 * 224, fr=2 * EMPTY + 2 * P, ft=2 * P),
+    BF: dict(xs=4 * P, ws=512 * O, ez=516, fv=64 * R, ma=3 * SEG, mb=2 * SEG, sg=192, sh=192, rk=2 * SEG,
+             hg=4 * P, hf=4 * WIN, bt=512, fr=2 * EMPTY + 2 * P, ft=2 * P),
     I32: dict(nbr=72, sdr=8, pi=8, wy=2, wi=2, f1=2, f2=2, f3=2),
-    U16: dict(ids=16 * R, sdl=2, sl=24, gl=2, n9u=16, nbu=12, off=10, wl=4, fo=4, fu=24),
-    Q4: dict(first=P, stat=P, fw=608, fin=P, wq=128 * O, eq=512, new0=224, new1=224, new2=224, new3=224),
-    U8: dict(firsts=P, stats=P, fws=608, fins=P, wqs=128 * O, eqs=512, news0=224, news1=224, news2=224, news3=224),
-    F32: dict(pf=8, i128=128, i16=192, iz=144, dm=192, rs=192, mz=144, tri=32, tri0=32, s2=2, z32=32, slots=64, val=128 * R,
-              ct=36, jj=3, js=3, w16=24, jw=24, slb=24, gl0=5, rs3=9, rs48=144,
-              spot=EMPTY + NG, nbf=72, n9=16, n9a=16, n9b=16, gz=144, nbs=144, nbc=12, dn=9, g2=192, sp=192, fl=18, xx=18,
-              oo=18, uu=3, p8=9, dd=9, t2=9, t3=3, cand=3, t4=3, t5=3, zw0=536, zw1=536, gg=144, bb=144, ab=3, hi=6, ne=9,
-              ee=192, rr=480, rk3=3, pp=9, npp=1, ad=64, aa=192, at=192, wp=96, wx=2, pg=9, pas=3, tk=3, tk2=3, pd=3, pd2=3,
-              gb=128, f4=24, ys=O * P),
+    U16: dict(ids=16 * (R + 1), sdl=2, sl=24, gl=2, n9u=16, nbu=12, off=12, wl=4, fo=4, fu=24),
+    Q4: dict(first=P, stat=P, fw=800, fin=P, wq=128 * O, eq=512, new0=128),
+    U8: dict(firsts=P, stats=P, fws=800, fins=P, wqs=128 * O, eqs=512, new0s=128),
+    F32: dict(pf=8, i16=192, iz=144, x32=96, dm=192, rs=192, mz=144, tri=105, tri0=96, z80=80, slots=192, val=520,
+              jj=3, js=3, w16=24, jw=24, slb=24, gl0=6, rs3=9,
+              spot=EMPTY + NG, nbf=72, n9=16, n9a=16, n9b=16, gz=144, nbs=144, nbc=12, dn=9, g2=192, sp=192,
+              uu=3, p8=9, dd=9, t2=9, thr=3, t4=3, t5=3, zw=3 * WIN, gg=240, bb=240, ab=3, ne=9,
+              ee=105, rr=480, rkf=291, cnt=1, pp=9, aa=192, at=192, wp=192, pg=9, pas=3, tk2=3, pd=3, pd2=3,
+              gb=128, f4=24, yb=64 * R, ys0=EMPTY + NG, ys1=EMPTY + NG),
 }
 SCRATCH = {n: ("sbuf", [128, w], d) for d, b in _BUF.items() for n, w in b.items()}
-SCRATCH["pz"] = ("psum", [128, 512 * 3], F32)
+SCRATCH["pz"] = ("psum", [128, 512 * 4], F32)
 SCRATCH["pe"] = ("psum", [128, 512 * 4], F32)
 
 SEMAPHORES = ["cv", "cs", "ct", "cg", "sent", "lx", "lw", "lnb", "lsd", "st"] + \
@@ -130,42 +132,41 @@ def rank_program(g, core, T, topo):
         run("v", lambda: g.vector.memset(out[0], c), [out], [])
 
     def scan(out, d0, d1, op0, op1, init=0.0):
-        run("v", lambda: g.vector.tensor_tensor_scan(out[0], d0[0], d1[0], init, op0, op1), [out], [d0, d1])
+        run("v", lambda: g.vector.tensor_tensor_scan(out[0], d0[0], d1[0], ap(init), op0, op1), [out], [d0, d1, init])
 
     def tr(out, in_):
         run("v", lambda: g.vector.transpose(out[0], in_[0]), [out], [in_])
 
     def quant(name, a, n, in_):
-        out, sc = W(name[0], a, n), W(name[1], a, n)
+        out, sc = W(name, a, n), W(name + "s", a, n)
         run("v", lambda: g.vector.quantize_mx(out[0], sc[0], in_[0]), [out, sc], [in_])
 
-    def act(out, in_, func=AF.Identity, bias=None, scale=None):
-        kw = {}
+    def act(out, in_, func=AF.Identity, bias=None, scale=None, acc=None):
+        kw = {} if acc is None else {"accum_out": acc[0]}
         if bias is not None:
             kw["bias"] = ap(bias)
         if scale is not None:
             kw["scale"] = ap(scale)
-        run("s", lambda: g.scalar.activation(out[0], in_[0], func, **kw), [out], [in_, bias, scale])
+        run("s", lambda: g.scalar.activation(out[0], in_[0], func, **kw), [out] + ([acc] if acc else []), [in_, bias, scale])
 
     def mm(bank, k, lhs, a, rhs, b, n):
-        out, l, ls, r, rs = W(bank, 512 * k, n), W(lhs[0], a, 128), W(lhs[1], a, 128), W(rhs[0], b, n), W(rhs[1], b, n)
+        out, l, ls, r, rs = W(bank, 512 * k, n), W(lhs, a, 128), W(lhs + "s", a, 128), W(rhs, b, n), W(rhs + "s", b, n)
         run("t", lambda: g.tensor.matmul_mx(out[0], l[0], ls[0], r[0], rs[0], True, True), [out], [l, ls, r, rs])
 
     def iota(out, pattern, base, cm):
         run("g", lambda: g.iota(out[0], pattern, base, cm, allow_small_or_imprecise_dtypes=True), [out], [])
 
-    def loads(q, sem, pairs):
-        for out, src in pairs:
+    def loads(sem, items):
+        for q, out, src in items:
             Q[q].dma_start(out[0], src).then_inc(T.sem[sem], 16)
-        count[sem] = 16 * len(pairs)
-        for out, src in pairs:
-            note([], out[1], (sem, count[sem], dict(known[q])))
+        count[sem] = 16 * len(items)
+        for q, out, src in items:
+            note([], out[1], (sem, count[sem], {}))
 
     def store(q, dst, in_):
         run(q, lambda: Q[q].dma_start(dst, in_[0]), [], [in_], sem="st", inc=16)
 
-    FIRST, STAT, FW, FIN, WQ, EQ = [(n, n + "s") for n in ("first", "stat", "fw", "fin", "wq", "eq")]
-    NEW = [("new%d" % t, "news%d" % t) for t in range(R)]
+    NEW = [("new0", 0)] + [("fw", P + 128 * t) for t in range(R)]
     peers = [(rank + d) % N for d in range(1, N)]
     mask = -1
     for q in peers:
@@ -187,12 +188,13 @@ def rank_program(g, core, T, topo):
         send("ids", 16 * t + 6, 2, "aid%d" % t)
 
     def send_cols(t):
-        send(NEW[t][0], 96, 32, "acol%d" % t, u8)
-        send(NEW[t][1], 96, 32, "acol%d" % t)
+        send(NEW[t][0], NEW[t][1], 32, "acol%d" % t, u8)
+        send(NEW[t][0] + "s", NEW[t][1], 32, "acol%d" % t)
 
     for t in range(R):
+        nm, a = NEW[t]
         for views, sem, calls in (([W("ids", 16 * t + 8, 6)], "aid%d" % t, 1),
-                                  ([W(NEW[t][0], 128, 96), W(NEW[t][1], 128, 96)], "acol%d" % t, 2)):
+                                  ([W(nm, a + 32, 96), W(nm + "s", a + 32, 96)], "acol%d" % t, 2)):
             count[sem] = calls * (N - 1) * neng
             for v in views:
                 note([], v[1], (sem, count[sem], {}))
@@ -200,110 +202,100 @@ def rank_program(g, core, T, topo):
     quads = [(32 * a, 32 * a + 32) for a in range(4)]
     halves = [(0, 64), (64, 128)]
 
-    loads("y", "lx", [(V("xs"), T.x[:])])
-    loads("s", "lsd", [(V("sdr", 0, 2, p=(0, 16)), T.sd[:]), (V("sdr", 0, 2, p=(16, 32)), T.sd[:])])
-    loads("y", "lnb", [(V("nbr", p=(0, 16)), T.nb[:]), (V("nbr", p=(16, 32)), T.nb[:])])
+    loads("lsd", [("y", V("sdr", 0, 2, p=(0, 16)), T.sd[:]), ("s", V("sdr", 0, 2, p=(16, 32)), T.sd[:])])
+    loads("lx", [("y", V("xs"), T.x[:])])
+    loads("lnb", [("s", V("nbr", p=(0, 16)), T.nb[:]), ("s", V("nbr", p=(16, 32)), T.nb[:])])
     need("y", ("acol0", count["acol0"], {}))
-    loads("y", "lw", [(V("ws"), T.w[:])])
+    loads("lw", [("y", V("ws"), T.w[:])])
 
     run("g", lambda: g.iota(T.pi[:, 0:1], [[0, 1]], 0, 1), [W("pi", 0, 1)], [])
-    iota(V("i128"), [[1, 128]], 0, 0)
-    iota(V("spot", 0, SPW // 2), [[-1, SPW // 2]], -1, 0)
+    iota(V("val"), [[1, 520]], POS, 0)
     iota(V("i16"), [[0, 12], [1, 16]], 0, 0)
-    ms(V("zb"), 0.0)
-    act(W("et", 0, 1024), V("zb"))
-    act(W("et", 1024, 1024), V("zb"))
+    iota(V("iz"), [[0, 3], [1, 16], [0, 3]], 0, 0)
+    ms(V("z80"), 0.0)
+    ms(V("rs3"), 0.0)
+    ms(V("ne"), 0.0)
+    ms(W("bt", 0, 384), 0.0)
     p0 = W("pi", 0, 1)
     ts(W("pi", 1, 1), p0, 15, A.bitwise_and)
     ts(W("pi", 2, 1), p0, 4, A.logical_shift_right)
     ts(W("pi", 3, 1), p0, 31, A.bitwise_and)
     ts(W("pi", 4, 1), p0, 5, A.logical_shift_right, 1, A.bitwise_and)
     ts(W("pi", 5, 1), p0, 6, A.logical_shift_right)
-    ms(V("zw0", OLD, 536), NEG)
+    ms(V("rs3", 0, 9, 3), 9 * NEG)
     cp(W("pf", 0, 6), W("pi", 0, 6))
     pf, r16, grp, u32c, odd, upper = [W("pf", i, 1) for i in range(6)]
-    ms(V("zw1", NEGC, 536), NEG)
-    ms(V("rs3"), 0.0)
-    ms(V("rs48"), 0.0)
-    ts(V("eye"), V("i128"), pf, A.is_equal)
-    ts(W("gl0", 4, 1), r16, 3.0, A.mult)
+    ms(V("ma", 192, 2 * SEG, SEG), 0.0)
+    ms(V("ma", 193, 2 * SEG, SEG), 0.0)
+    ms(W("mb", 192, 2), 0.0)
+    ms(W("mb", SEG + 192, 2), 0.0)
+    ts(W("gl0", 5, 1), pf, 4.0, A.mult, float(POS + 3), A.add)
     ts(W("gl0", 1, 1), r16, 3.0, A.is_ge, 21.0, A.mult)
     ts(W("gl0", 2, 1), r16, 6.0, A.is_ge, 21.0, A.mult)
     ts(W("gl0", 3, 1), grp, 3.0, A.mult, r16, A.add)
-    ts(V("tri0"), W("i128", 0, 32), u32c, A.is_gt, odd, A.subtract)
-    ts(V("s2"), W("pf", 4, 2), -STEP, A.mult, STEP, A.add)
-    ts(W("gl0", 0, 1), W("gl0", 1, 1), W("gl0", 2, 1), A.add, W("gl0", 3, 1), A.add)
-    ts(V("tri"), V("tri0"), STEP, A.mult)
-    ms(V("ne"), 0.0)
-    ts(W("gl", 0, 1), W("gl0", 0, 1), 71.0, A.min)
-    ms(V("z32"), 0.0)
-    ms(V("rs3", 0, 9, 3), 9 * NEG)
-    ms(V("rs48", 0, 144, 48), 9 * NEG)
-    ms(V("fl", 0, 18, 2), 0.0)
-    for c in range(2):
-        ms(V("ma", 192 + c, 3 * SEG, SEG), 0.0)
-        ms(V("mb", 192 + c, 3 * SEG, SEG), 0.0)
     for a in quads:
         cp(V("sdl", p=a), W("sdr", 0, 2, (0, 32)))
+    ts(W("gl0", 0, 1), W("gl0", 1, 1), W("gl0", 2, 1), A.add, W("gl0", 3, 1), A.add)
     ts(W("ids", 6, 2), V("sdl"), float(P * rank), A.add)
-    act(V("spot", SPW // 2, SPW), V("spot", 0, SPW // 2), bias=float(-(SPW // 2)))
     send_ids(0)
-    iota(V("iz"), [[0, 3], [1, 16], [0, 3]], 0, 0)
     iota(V("slb"), [[1, 3], [48, 8]], 0, 0)
     iota(V("jj"), [[1, 3]], P * rank, 3)
+    ts(W("gl", 0, 1), W("gl0", 0, 1), 71.0, A.min)
+    for i in range(3):
+        act(W("spot", 520 * i, 520), V("val"), bias=float(POS - 1 - 520 * i), scale=-1.0)
+    for c in range(3):
+        act(W("gg", 80 * c + 48, 32), W("z80", 0, 32), bias=NEG)
+        act(W("zw", WIN * c, POS), W("z80", 0, POS), bias=NEG)
     for b in range(4):
-        act(V("et", 512 * b + b, 512 * b + 512, 4), V("eye"))
+        act(W("hf", WIN * b, POS), W("z80", 0, POS))
+    ts(V("ez"), W("val", 0, 516), W("gl0", 5, 1), A.is_equal)
     for a in quads:
         cp(V("nbf", p=a), V("nbr", p=(0, 32)))
+    quant("eq", 0, 128, W("ez", 3, 512))
     cp(V("n9"), ind(V("nbf"), W("gl", 0, 1)))
-    ts(V("dm"), V("i16"), r16, A.not_equal, 2 * NEG, A.mult)
+    quant("eq", 128, 128, W("ez", 2, 512))
     ts(V("n9a"), V("n9"), 0.0, A.is_lt, float(NONE + 1), A.mult)
-    quant(FIRST, 0, P, V("xs"))
-    cp(u32(W("new0", 96, 32)), ind(u32(V("first")), V("sdl")))
-    act(W("news0", 96, 32), ind(V("firsts"), V("sdl")), AF.Copy)
-    send_cols(0)
-    iota(V("ct"), [[-128, 4], [80, 3], [-16, 3]], -(OLD + 15), 0)
-    iota(V("xx", 1, 18, 2), [[48, 3], [16, 3]], OLD + 15 - NEGC, 0)
-    iota(V("js"), [[1 << SH, 3]], 0, 3 << SH)
-    iota(V("slots"), [[16, 2], [0, 2], [1, 16]], 0, 0)
-    iota(V("bt"), [[0, 4 * 224]], 0, 0)
-    iota(V("w16"), [[16, 24]], -(P - 1), 0)
-    iota(V("fv"), [[32, 4], [0, 2], [1, 32]], 1, 0)
-    iota(V("val", 128, 128 * R), [[1, 128 * (R - 1)]], 128, 0)
+    quant("eq", 256, 128, W("ez", 1, 512))
     tt(V("n9b"), V("n9a"), V("n9"), A.add)
-    ts(V("sl"), V("slb"), W("gl0", 4, 1), A.add)
-    ts(V("mz"), V("iz"), r16, A.not_equal, 2 * NEG, A.mult)
+    quant("eq", 384, 128, W("ez", 0, 512))
     cp(V("n9u"), V("n9b"))
-    quant(EQ, 0, 512, V("et"))
+    ts(V("mz"), V("iz"), r16, A.not_equal, 2 * NEG, A.mult)
+    ts(W("gl0", 4, 1), r16, 3.0, A.mult)
+    quant("first", 0, P, V("xs"))
+    cp(u32(W("new0", 0, 32)), ind(u32(V("first")), V("sdl")))
+    act(W("new0s", 0, 32), ind(V("firsts"), V("sdl")), AF.Copy)
+    send_cols(0)
+    iota(V("x32"), [[0, 3], [1, 32]], 0, 0)
+    iota(V("js"), [[1 << SH, 3]], 0, 3 << SH)
+    iota(V("slots"), [[16, 2], [0, 6], [1, 16]], 0, 0)
+    iota(V("w16"), [[16, 24]], -(P + MID), 0)
+    iota(V("fv"), [[128, 4], [0, 2], [1, 32]], -MID, 0)
+    iota(V("fr", 0, 2 * P), [[0, 2 * P]], -1024, 0)
+    ts(V("sl"), V("slb"), W("gl0", 4, 1), A.add)
+    tt(V("gz"), ind(V("spot", 0, SPW), W("n9u", 0, 9)), V("mz"), A.add)
     for b in range(4):
-        mm("pe", b, EQ, 128 * b, FIRST, 0, P)
+        mm("pe", b, "eq", 128 * b, "first", 0, P)
     act(V("stats"), ind(V("firsts"), V("sl")), AF.Copy)
     for b in range(4):
         act(W("hg", P * b, P), W("pe", 512 * b, P), scale=0.5)
-    tt(V("gz"), ind(V("spot", 0, SPW), W("n9u", 0, 9)), V("mz"), A.add)
     ts(V("rs"), V("i16"), 0.0, A.is_equal, 9 * NEG, A.mult)
-    cp(ind(V("spot"), W("ids", 6, 8)), V("i128"))
+    ts(V("dm"), V("i16"), r16, A.not_equal, 2 * NEG, A.mult)
     for c in range(3):
         scan(W("nbs", 48 * c, 48), W("rs", 0, 48), V("gz", c, 144, 3), A.add, A.max)
     cp(W("nbu", 9, 3), V("jj"))
     for k in range(M):
-        ts(V("nbu", 2 - k, 9, 3), V("nbs", 16 * k + 15, 144, 48), -1.0, A.mult, -1.0, A.add)
+        ts(V("nbu", k, 9, 3), V("nbs", 16 * k + 15, 144, 48), -1.0, A.mult, -1.0, A.add)
     cp(u32(V("stat")), ind(u32(V("first")), V("sl")))
+    cp(ind(V("spot"), W("ids", 6, 8)), W("val", 0, 128))
 
-    def later(t):
-        if t == 0:
-            cp(V("nbc"), V("nbu"))
-            ts(V("pd"), V("jj"), 1.0, A.add)
-            ms(V("fr", 0, 2 * P), -1024.0)
-            tt(W("dn", 0, 8), W("nbc", 0, 8), W("nbc", 1, 8), A.subtract)
-            tt(V("pd2"), V("pd"), V("uu"), A.mult)
-            ts(V("dn", 2, 9, 3), V("nbc", 2, 9, 3), 1.0, A.add)
-            tt(V("pas"), V("jj"), V("pd2"), A.subtract)
-        if t == 1:
-            quant(FW, 0, P, V("xs"))
-        if t == 2:
-            quant(WQ, 0, 128 * O, V("ws"))
-            ts(V("jw"), V("w16"), r16, A.add)
+    def products(t):
+        for o in range(O):
+            mm("pz", o, "wq", 128 * o, "fw", NEW[t + 1][1] - 96, 128)
+        for o in range(O):
+            act(W("yb", 64 * t + 32 * o, 32), W("pz", 512 * o + 96, 32))
+
+    def place_y(t, o):
+        cp(ind(V("ys%d" % o), W("ids", 16 * t + 22, 2)), W("yb", 64 * t + 32 * o, 32))
 
     def parents():
         for c in range(3):
@@ -313,130 +305,191 @@ def rank_program(g, core, T, topo):
         cp(ind(V("fr"), V("fo")), W("fv", 64 * t, 64))
 
     for t in range(R):
-        zw, zn, last = "zw%d" % (t % 2), "zw%d" % ((t + 1) % 2), t == R - 1
+        last = t == R - 1
+        nm, a0 = NEW[t]
         n = 12 if t == 0 else 9
         if t > 0:
-            cp(ind(V("spot"), W("ids", 16 * t + 6, 8)), W("val", 128 * t, 128))
+            cp(ind(V("spot"), W("ids", 16 * t + 8, 6)), W("val", 128 * t + 32, 96))
         tt(W("g2", 0, 16 * n), ind(V("spot", 0, SPW), W("nbu", 0, n)), W("dm", 0, 16 * n), A.add)
-        scan(W("sp", 0, 16 * n), W("rs", 0, 16 * n), W("g2", 0, 16 * n), A.add, A.max)
-        sp9 = V("sp", 15, 144, 16)
-        ts(V("fl", 1, 18, 2), sp9, float(128 * t), A.is_ge)
-        tt(V("xx", 0, 18, 2), sp9, W("ct", 9 * t, 9), A.add)
         if t == 0:
+            ts(V("tri0"), V("x32"), u32c, A.is_gt, odd, A.subtract)
+        scan(W("sp", 0, 16 * n), W("rs", 0, 16 * n), W("g2", 0, 16 * n), A.add, A.max)
+        if t == 0:
+            cp(V("nbc"), V("nbu"))
             ts(V("uu"), V("sp", 159, 192, 16), 0.0, A.is_lt)
-        scan(V("t2"), V("rs3"), sp9, A.add, A.max)
-        scan(V("oo"), V("fl"), V("xx"), A.mult, A.add)
-        ts(V("t3"), V("t2", 2, 9, 3), 0.0, A.is_ge)
+            ts(W("tri", 0, 96), V("tri0"), STEP, A.mult)
         for c in range(3):
-            ts(W("off", 3 * c, 3), V("oo", 6 * c + 1, 6 * c + 6, 2), W("uu", c, 1), A.mult, float(NEGC), A.add)
+            ts(W("off", 4 * c, 3), V("sp", 48 * c + 15, 48 * c + 48, 16), W("uu", c, 1), A.mult, 0.0, A.max)
         for c in range(3):
             act(W("p8", 3 * c, 3), V("sp", 48 * c + 15, 48 * c + 48, 16), AF.Relu, scale=W("uu", c, 1))
-        tt(V("cand"), V("t3"), V("uu"), A.mult)
-        for c in range(3):
-            mm("pz", c, STAT, 128 * c, NEW[t], 96, 128)
-        for b in range(4):
-            mm("pe", b, EQ, 128 * b, NEW[t], 96, 128)
-        act(W(zw, 0, 128), W("pz", 0, 128), bias=TINY)
-        ts(W(zw, 128, 128), W("pz", 512, 128), TINY, A.add)
-        act(W(zw, 256, 128), W("pz", 1024, 128), bias=TINY)
+        if t == 0:
+            for c in range(3):
+                ts(V("tri", 96 + c, 102, 3), W("pf", 4, 2), -STEP, A.mult, STEP, A.add)
+            ts(W("tri", 102, 3), W("z80", 0, 3), upper, A.subtract, STEP, A.mult)
+        if t == 1:
+            quant("wq", 0, 128 * O, V("ws"))
+        if t == 2:
+            place_y(0, 0)
+            place_y(0, 1)
+        if t == 3:
+            quant("fw", 0, P, V("xs"))
+        scan(V("t2"), V("rs3"), V("p8"), A.add, A.max)
         tt(V("t4"), V("p8", 2, 9, 3), V("js"), A.add)
-        tt(V("gg"), ind(V(zw), W("off", 0, 9)), W("dm", 0, 144), A.add)
-        ts(V("t5"), V("cand"), -float(EMPTY << SH), A.mult, float(EMPTY << SH), A.add)
-        scan(V("bb"), V("rs48"), V("gg"), A.add, A.max)
-        vc = [W("bb", 48 * c + 47, 1) for c in range(3)]
-        act(V("ab"), V("bb", 47, 144, 48), AF.Abs)
-        for c in range(3):
-            act(W("ee", 32 * c, 32), V("z32"), bias=vc[c])
-        scan(W(zn, OLD, 144), W("rs", 0, 144), V("gg"), A.add, A.max)
-        for c in range(3):
-            ts(W("ee", 96 + 32 * c, 32), V("tri"), W("ab", c, 1), A.mult, vc[c], A.add)
-        for c in range(3):
-            act(W("hi", 2 * c, 2), V("s2"), bias=vc[c], scale=W("ab", c, 1))
         tt(W("dd", 0, 8), W("p8", 0, 8), W("p8", 1, 8), A.subtract)
-        tr(W("rr", 0, 192), V("ee"))
-        ts(W("ma", SEG + 192, 1), vc[0], vc[1], A.is_equal)
-        cp(W("rr", 192, 96, quads[0]), W("rr", 0, 96, quads[1]))
-        act(W("rr", 192, 96, quads[2]), W("rr", 0, 96, quads[3]))
-        cp(W("rr", 192, 96, quads[1]), W("rr", 0, 96, quads[0]))
-        act(W("rr", 192, 96, quads[3]), W("rr", 0, 96, quads[2]))
-        for h in range(2):
-            act(W("rr", 288, 96, halves[h]), W("rr", 0, 96, halves[1 - h]))
-        for h in range(2):
-            act(W("rr", 384, 96, halves[h]), W("rr", 192, 96, halves[1 - h]))
-        act(V("sg"), W("rr", 288, 192), AF.Sign, bias=W("hi", 5, 1), scale=-1.0)
-        act(W("ne", 1, 2), V(zn, OLD + 31, OLD + 48, 16), AF.Sign, bias=vc[0], scale=-1.0)
-        act(W("mb", 2 * SEG, 192), V("sg"), AF.Relu)
-        for c in range(1, 3):
-            act(W("ne", 3 * c + 1, 2), V(zn, OLD + 48 * c + 31, OLD + 48 * c + 48, 16), AF.Sign, bias=vc[c], scale=-1.0)
+        ts(V("t5"), V("t2", 2, 9, 3), 1.0, A.is_lt, float(EMPTY << SH), A.mult)
+        ts(V("thr"), V("t2", 2, 9, 3), 1.0, A.is_ge, float(K), A.mult)
+        if t > 1:
+            place_y(t - 1, 0)
         tt(V("dd", 2, 9, 3), V("t4"), V("t5"), A.add)
+        if t > 1:
+            place_y(t - 1, 1)
         for c in range(3):
-            ts(W("ma", SEG * c, 192), W("rr", 96, 192), W("hi", 2 * c, 1), A.is_ge)
-        ts(W("ma", 2 * SEG + 192, 2), V("bb", 47, 96, 48), vc[2], A.is_equal)
-        for c in range(2):
-            ts(W("mb", SEG * c, 192), W("rr", 288, 192), W("hi", 2 * c + 1, 1), A.is_ge)
+            mm("pz", c, "stat", 128 * c, nm, a0, 128)
+        for b in range(4):
+            mm("pe", b, "eq", 128 * b, nm, a0, 128)
         for c in range(3):
-            scan(W("rk", SEG * c, SEG), W("ma", SEG * c, SEG), W("mb", SEG * c, SEG),
-                 A.add, A.add if c < 2 else A.subtract, 0.0 if c < 2 else 192.0)
-        scan(V("pp"), V("ne"), V("dd"), A.mult, A.add)
-        cp(V("rk3"), V("rk", SEG - 1, 3 * SEG, SEG))
-        act(W("hf", 128 * t, 128), W("pe", 0, 128), scale=0.5)
-        act(V("npp"), W("pp", 8, 1), scale=-1.0)
-        act(V("ad"), V("slots"), AF.Abs, bias=W("rk", 3 * SEG - 1, 1), scale=-1.0)
-        for m in range(2):
-            act(W("aa", 96 * m + 64, 32), W("ad", 32 * m, 32), AF.Relu, bias=W("pp", 8, 1), scale=V("npp"))
-        for b in range(1, 4):
-            act(W("hf", 512 * b + 128 * t, 128), W("pe", 512 * b, 128), scale=0.5)
-        for c in range(2):
-            for m in range(2):
-                ts(W("aa", 96 * m + 32 * c, 32), W("slots", 32 * m, 32), W("rk3", c, 1), A.is_equal, W("pp", 3 * c + 2, 1), A.mult)
-        ts(V("tk"), V("rk3"), float(K), A.is_lt)
-        tr(V("at"), V("aa"))
-        tt(V("tk2"), V("tk"), V("cand"), A.mult)
-        for m in range(2):
-            scan(W("wp", 48 * m, 48), W("at", 96 * m, 48), W("at", 96 * m + 48, 48), A.add, A.add)
-        tt(V("wx", p=halves[0]), V("wp", 47, 96, 48, p=halves[0]), V("wp", 47, 96, 48, p=halves[1]), A.add)
-        for a in quads:
-            tt(V("wy", p=a), V("wx", p=quads[0]), V("wx", p=quads[1]), A.add)
-        ts(W("wl", 0, 2), V("wy"), 2.0 ** -SH, A.mult, float(P - 1), A.min)
-        if not last:
-            ts(W("ids", 16 * t + 22, 2), V("wy"), 2.0 ** -SH, A.mult, float(P * rank), A.add)
-            send_ids(t + 1)
-        ts(V("wi"), V("wy"), 511, A.bitwise_and)
-        for b in range(4):
-            act(W("gb", 32 * b, 32), ind(W("hg", P * b, P), W("wl", 0, 2)))
-        ts(V("f1"), V("wy"), SH, A.logical_shift_right, 15, A.bitwise_and)
-        cp(W("wl", 2, 2), V("wi"))
-        ts(V("f2"), V("wy"), SH - 1, A.logical_shift_right)
-        for b in range(4):
-            tt(V("bt", 384 + b, 512, 4), ind(W("hf", 512 * b, 128 * t + 128), W("wl", 2, 2)), W("gb", 32 * b, 32), A.add)
-        if not last:
-            quant(NEW[t + 1], 0, 128, W("bt", 0, 512))
-            send_cols(t + 1)
-            later(t)
-        tt(V("f3"), V("f2"), V("f1"), A.subtract)
-        scan(V("pg"), V("ne"), V("dn"), A.mult, A.add)
-        for d in range(2):
-            ts(W("fo", 2 * d, 2), V("f3"), float(16 * d), A.add)
-        parents()
-        quant(FW, P + 32 * t, 128, W("bt", 384, 512))
-        mark(t)
-        if not last:
-            tt(V("uu"), V("uu"), V("tk2"), A.subtract)
+            act(W("zw", WIN * c + POS + 128 * t, 128), W("pz", 512 * c, 128), bias=TINY)
 
-    store("y", T.pa[:], V("pas"))
+        def gather(c):
+            tt(W("gg", 80 * c, 48), ind(W("zw", WIN * c, POS + 128 * t + 128), W("off", 4 * c, 3)), W("dm", 0, 48), A.add)
+
+        def best(c):
+            scan(V("bb", c, 240, 3), V("z80"), W("gg", 80 * c, 80), A.add, A.max, 9 * NEG)
+        gather(0)
+        gather(1)
+        best(0)
+        gather(2)
+        best(1)
+        best(2)
+        vc = [W("bb", 141 + c, 1) for c in range(3)]
+        hi = lambda c, h: W("ee", 96 + 3 * h + c, 1)
+        for c in range(4):
+            if c < 3:
+                act(W("ab", c, 1), vc[c], AF.Abs)
+            if c > 0:
+                act(V("ee", c - 1, 105, 3), V("tri", c - 1, 105, 3), bias=vc[c - 1], scale=W("ab", c - 1, 1))
+        tr(W("rr", 384, 96), W("bb", 144, 96))
+        tt(V("ne", 1, 9, 3), W("bb", 45, 3), W("bb", 141, 3), A.is_equal)
+        cp(W("rr", 96, 96, quads[0]), W("rr", 384, 96, quads[1]))
+        cp(W("rr", 96, 96, quads[1]), W("rr", 384, 96, quads[0]))
+        act(W("rr", 96, 96, quads[2]), W("rr", 384, 96, quads[3]))
+        act(W("rr", 96, 96, quads[3]), W("rr", 384, 96, quads[2]))
+        tr(W("rr", 0, 96), W("ee", 0, 96))
+        for h in range(2):
+            act(W("rr", 192, 96, halves[h]), W("rr", 384, 96, halves[1 - h]))
+        for h in range(2):
+            act(W("rr", 288, 96, halves[h]), W("rr", 96, 96, halves[1 - h]))
+        act(V("sg"), W("rr", 192, 192), AF.Sign, bias=hi(2, 2), scale=-1.0)
+        act(V("sh"), V("sg"), AF.Relu, scale=-1.0, acc=V("cnt"))
+        tt(V("ne", 2, 9, 3), W("bb", 93, 3), W("bb", 141, 3), A.is_equal)
+        ts(W("ma", SEG + 192, 1), vc[0], vc[1], A.is_equal)
+
+        def ahead(row, c, h):
+            ts(W(row, SEG * c, 192), W("rr", 192 * h, 192), hi(c, h), A.is_ge)
+
+        def rank_of(c):
+            scan(W("rk", SEG * c, SEG), W("ma", SEG * c, SEG), W("mb", SEG * c, SEG), A.add, A.add)
+            act(W("rkf", 288 + c, 1), W("rk", SEG * c + SEG - 1, 1))
+        ahead("ma", 0, 0)
+        ahead("ma", 1, 0)
+        ahead("mb", 0, 1)
+        ts(W("ma", 2 * SEG + 192, 2), W("bb", 141, 2), vc[2], A.is_equal)
+        ahead("mb", 1, 1)
+        rank_of(0)
+        ahead("ma", 2, 0)
+        rank_of(1)
+        scan(V("pp"), V("ne"), V("dd"), A.mult, A.add)
+        scan(V("rkf", 2, 291, 3), W("ma", 2 * SEG, 97), W("ma", 2 * SEG + 97, 97), A.add, A.add, V("cnt"))
+        for c in (0, 2, 1):
+            ts(V("aa", c, 192, 3), V("slots", c, 192, 3), W("rkf", 288 + c, 1), A.is_equal, W("pp", 3 * c + 2, 1), A.mult)
+        for b in range(4):
+            act(W("hf", WIN * b + POS + 128 * t, 128), W("pe", 512 * b, 128), scale=0.5)
+        if t == 1:
+            products(0)
+            for o in range(O):
+                mm("pz", 2 + o, "wq", 128 * o, "first", 0, P)
+                act(W("ys%d" % o, P * rank, P), W("pz", 512 * (2 + o), P))
+        if t == 0:
+            ts(V("pd"), V("jj"), 1.0, A.add)
+        tr(V("at"), V("aa"))
+        tt(V("tk2"), W("rkf", 288, 3), V("thr"), A.is_lt)
+        if t == 0:
+            tt(V("pd2"), V("pd"), V("uu"), A.mult)
+        else:
+            scan(V("pg"), V("ne"), V("dn"), A.mult, A.add)
+        for m in range(2):
+            scan(W("wp", 96 * m, 96, halves[0]), W("at", 96 * m, 96, halves[0]), W("at", 96 * m, 96, halves[1]), A.add, A.add)
+        for a in quads:
+            tt(V("wy", p=a), V("wp", 95, 192, 96, p=quads[0]), V("wp", 95, 192, 96, p=quads[1]), A.add)
+
+        def ids():
+            ts(W("ids", 16 * t + 22, 2), V("wy"), 2.0 ** -SH, A.mult, float(P * rank), A.add)
+
+        def f12(i):
+            if i == 1:
+                ts(V("f1"), V("wy"), SH, A.logical_shift_right, 15, A.bitwise_and)
+            else:
+                ts(V("f2"), V("wy"), SH - 1, A.logical_shift_right)
+
+        def fo():
+            for d in range(2):
+                ts(W("fo", 2 * d, 2), V("f3"), float(16 * d), A.add)
+        ts(W("wl", 0, 2), V("wy"), 2.0 ** -SH, A.mult, float(P - 1), A.min)
+        ts(V("wi"), V("wy"), 1023, A.bitwise_and)
+        if not last:
+            ids()
+            send_ids(t + 1)
+            tt(V("uu"), V("uu"), V("tk2"), A.subtract)
+        else:
+            f12(1)
+            f12(2)
+        for b in range(3):
+            act(W("gb", 32 * b, 32), ind(W("hg", P * b, P), W("wl", 0, 2)))
+        if t > 0:
+            parents()
+        cp(W("wl", 2, 2), V("wi"))
+        cp(W("gb", 96, 32), ind(W("hg", P * 3, P), W("wl", 0, 2)))
+        if last:
+            tt(V("f3"), V("f2"), V("f1"), A.subtract)
+            store("y", T.pa[:], V("pas"))
+        for b in (0, 1, 3, 2):
+            tt(V("bt", 384 + b, 512, 4), ind(W("hf", WIN * b, POS + 128 * t + 128), W("wl", 2, 2)), W("gb", 32 * b, 32), A.add)
+        if last:
+            fo()
+        else:
+            f12(1)
+            f12(2)
+        quant("fw", NEW[t + 1][1] - 96, 128, V("bt"))
+        if not last:
+            send_cols(t + 1)
+            cp(ind(V("spot"), W("ids", 16 * t + 22, 2)), W("val", 128 * t + 128, 32))
+            tt(V("f3"), V("f2"), V("f1"), A.subtract)
+            if t == 0:
+                tt(W("dn", 0, 8), W("nbc", 0, 8), W("nbc", 1, 8), A.subtract)
+                tt(V("pas"), V("jj"), V("pd2"), A.subtract)
+                ts(V("dn", 2, 9, 3), V("nbc", 2, 9, 3), 1.0, A.add)
+            if t == 2:
+                ts(V("jw"), V("w16"), r16, A.add)
+            fo()
+            if t == 0:
+                scan(V("pg"), V("ne"), V("dn"), A.mult, A.add)
+                parents()
+        if t > 0:
+            products(t)
+        mark(t)
+
+    ids()
     tr(V("ft"), W("fr", 0, 2 * P))
+    place_y(R - 1, 0)
+    store("y", T.y[:, 0:P], W("ys0", P * rank, P))
     tt(V("f4"), V("ft", 0, 2 * P, 32), V("jw"), A.max)
-    ts(V("fu"), V("f4"), float(P - 1), A.add)
+    place_y(R - 1, 1)
+    store("s", T.y[:, P:2 * P], W("ys1", P * rank, P))
+    ts(V("fu"), V("f4"), float(P + MID), A.add)
     cp(u32(V("fin")), ind(u32(V("fw")), V("fu")))
     act(V("fins"), ind(V("fws"), V("fu")), AF.Copy)
-    for o in range(O):
-        mm("pz", o, WQ, 128 * o, FIN, 0, P)
     store("y", T.oc[:], u8(V("fin")))
     for k in range(4):
-        store("y", T.osc[4 * k:4 * k + 4, :], V("fins", p=(32 * k, 32 * k + 4)))
-    act(W("ys", 0, P), W("pz", 0, P))
-    store("s", T.y[:, 0:P], W("ys", 0, P))
-    cp(W("ys", P, P), W("pz", 512, P))
-    store("y", T.y[:, P:2 * P], W("ys", P, P))
+        store("s" if k % 2 else "y", T.osc[4 * k:4 * k + 4, :], V("fins", p=(32 * k, 32 * k + 4)))
     for sem, val in count.items():
         g.wait_ge(T.sem[sem], val)

@@ -4,31 +4,31 @@ from concourse.mybir import dt, AluOpType, ActivationFunctionType
 N, P, S, K, R, M, O = 4, 384, 32, 32, 4, 3, 2
 F32, BF, I32, U16, Q4, U8 = "float32", "bfloat16", "int32", "uint16", "float8_e4m3fn_x4", "uint8"
 NG = N * P
-NONE = NG
-SPW = NG + 16
-EMPTY = 2048
-SH = 14
-POS = 8
+LEAD = 16
+SPW = NG + LEAD
+SH = 12
+CAND = SPW << SH
+POS = 1
 WIN = 528
-NEG = -1e29
+BIG = 2.0 ** 96
 SEG = 194
 TINY = 2.0 ** -80
 STEP = 2.0 ** -24 * (1 + 2.0 ** -8)
-MID = 208
+X0 = 96 + 32 * R
+MID = X0 + 128
 
 _BUF = {
-    BF: dict(xs=4 * P, ws=512 * O, ez=516, fv=64 * R, ma=3 * SEG, mb=2 * SEG, sg=192, sh=192, rk=2 * SEG,
-             hg=4 * P, hf=4 * WIN, bt=512, fr=2 * EMPTY + 2 * P, ft=2 * P),
-    I32: dict(nbr=72, sdr=8, pi=8, wy=2, wi=2, f1=2, f2=2, f3=2),
-    U16: dict(ids=16 * (R + 1), sdl=2, sl=24, gl=2, n9u=16, nbu=12, off=12, wl=4, fo=4, fu=24),
-    Q4: dict(first=P, stat=P, fw=800, fin=P, wq=128 * O, eq=512, new0=128),
-    U8: dict(firsts=P, stats=P, fws=800, fins=P, wqs=128 * O, eqs=512, new0s=128),
-    F32: dict(pf=8, i16=192, iz=144, x32=96, dm=192, rs=192, mz=144, tri=105, tri0=96, z80=80, slots=192, val=520,
-              jj=3, js=3, w16=24, jw=24, slb=24, gl0=6, rs3=9,
-              spot=EMPTY + NG, nbf=72, n9=16, n9a=16, n9b=16, gz=144, nbs=144, nbc=12, dn=9, g2=192, sp=192,
-              uu=3, p8=9, dd=9, t2=9, thr=3, t4=3, t5=3, zw=3 * WIN, gg=240, bb=240, ab=3, ne=9,
-              ee=105, rr=480, rkf=291, cnt=1, pp=9, aa=192, at=192, wp=192, pg=9, pas=3, tk2=3, pd=3, pd2=3,
-              gb=128, f4=24, yb=64 * R, ys0=EMPTY + NG, ys1=EMPTY + NG),
+    BF: dict(xs=4 * P + 128, ws=512 * O, ez=516, fv=32 * R, ma=5 * SEG + 2, sg=192, sh=192, rk=2 * SEG,
+             hg=4 * P, hf=4 * WIN, fr=2 * SPW + 16, ft=2 * P + 32),
+    I32: dict(nbr=72, sdr=2, sda=8, pi=8, wy=2, wi=2),
+    U16: dict(ids=16 * (R + 1), sdl=2, sdu=6, sl=24, gl=2, n9=16, off=12, wl=4, fl=2, fu=32),
+    Q4: dict(first=X0 + P, stat=P, fw=96 + 128 * (R - 1), fin=P, wq=128 * O, eq=512, new0=128),
+    U8: dict(firsts=X0 + P, stats=P, fws=96 + 128 * (R - 1), fins=P, wqs=128 * O, eqs=512, new0s=128),
+    F32: dict(pf=12, pn=1, ea=128, iz=192, x32=105, dm=48, rs=64, mz=192, tri=105, nk=80, slots=192, val=520,
+              jj=3, dio=3, fxd=3, cap=240, slb=24, i3=3, i2=2, gl0=6,
+              spot=2 * SPW, g2=192, sp=192, gz=144, nbs=192, dn=12, dd=12, thr=3,
+              zw=3 * WIN, gg=240, bb=240, ab=3, ne=12 * R, ee=105, rr=480, rkf=294, cnt=1, pp=12, aa=192, at=192, wp=192,
+              pg=12 * R, pas=3, tk=15, gb=128, yb=64 * R, ys0=2 * SPW, ys1=2 * SPW),
 }
 SCRATCH = {n: ("sbuf", [128, w], d) for d, b in _BUF.items() for n, w in b.items()}
 SCRATCH["pz"] = ("psum", [128, 512 * 4], F32)
@@ -166,7 +166,7 @@ def rank_program(g, core, T, topo):
     def store(q, dst, in_):
         run(q, lambda: Q[q].dma_start(dst, in_[0]), [], [in_], sem="st", inc=16)
 
-    NEW = [("new0", 0)] + [("fw", P + 128 * t) for t in range(R)]
+    NEW = [("new0", 0)] + [("fw", 96 + 128 * t) for t in range(R - 1)]
     peers = [(rank + d) % N for d in range(1, N)]
     mask = -1
     for q in peers:
@@ -174,18 +174,21 @@ def rank_program(g, core, T, topo):
     neng = bin(mask).count("1")
     dst_ids = [DstId(rid=topo.addr(T.cores[q])[0], pnc=topo.addr(T.cores[q])[1]) for q in peers]
 
-    def send(name, a, n, sem, cast=None):
+    def send(name, a, n, sem, cast=None, to=None):
         view = (lambda v: cast(v)) if cast else (lambda v: v)
         src = view(W(name, a, n))
         for ev in hazards(src[1], []):
             need("g", ev)
         x = RemoteDMATransfer(dst_ids=dst_ids, dma_engine_mask=mask, remote_sem=T.sem[sem], srcs=[src[0]],
-                              dsts=[view(W(name, a + n * ((rank - q) % N), n))[0] for q in peers])
+                              dsts=[view(W(to or name, a + n * ((rank - q) % N), n))[0] for q in peers])
         g.remote_dma_fused([x], local_sem=T.sem.sent)
         count["sent"] = count.get("sent", 0) + neng
 
     def send_ids(t):
-        send("ids", 16 * t + 6, 2, "aid%d" % t)
+        if t == 0:
+            send("sdr", 0, 2, "aid0", to="sda")
+        else:
+            send("ids", 16 * t + 6, 2, "aid%d" % t)
 
     def send_cols(t):
         send(NEW[t][0], NEW[t][1], 32, "acol%d" % t, u8)
@@ -193,7 +196,7 @@ def rank_program(g, core, T, topo):
 
     for t in range(R):
         nm, a = NEW[t]
-        for views, sem, calls in (([W("ids", 16 * t + 8, 6)], "aid%d" % t, 1),
+        for views, sem, calls in (([W("ids", 16 * t + 8, 6) if t else W("sda", 2, 6)], "aid%d" % t, 1),
                                   ([W(nm, a + 32, 96), W(nm + "s", a + 32, 96)], "acol%d" % t, 2)):
             count[sem] = calls * (N - 1) * neng
             for v in views:
@@ -201,293 +204,299 @@ def rank_program(g, core, T, topo):
 
     quads = [(32 * a, 32 * a + 32) for a in range(4)]
     halves = [(0, 64), (64, 128)]
+    mine = SPW + LEAD + P * rank
+    tile = W("xs", 4 * P - 384, 512)
 
     loads("lsd", [("y", V("sdr", 0, 2, p=(0, 16)), T.sd[:]), ("s", V("sdr", 0, 2, p=(16, 32)), T.sd[:])])
-    loads("lx", [("y", V("xs"), T.x[:])])
-    loads("lnb", [("s", V("nbr", p=(0, 16)), T.nb[:]), ("s", V("nbr", p=(16, 32)), T.nb[:])])
+    loads("lx", [("y", W("xs", 0, 4 * P), T.x[:])])
+    loads("lnb", [("ys"[a % 2], V("nbr", p=(16 * a, 16 * a + 16)), T.nb[:]) for a in range(4)])
     need("y", ("acol0", count["acol0"], {}))
     loads("lw", [("y", V("ws"), T.w[:])])
 
     run("g", lambda: g.iota(T.pi[:, 0:1], [[0, 1]], 0, 1), [W("pi", 0, 1)], [])
-    iota(V("val"), [[1, 520]], POS, 0)
-    iota(V("i16"), [[0, 12], [1, 16]], 0, 0)
-    iota(V("iz"), [[0, 3], [1, 16], [0, 3]], 0, 0)
-    ms(V("z80"), 0.0)
-    ms(V("rs3"), 0.0)
-    ms(V("ne"), 0.0)
-    ms(W("bt", 0, 384), 0.0)
+    iota(W("val", 0, 128), [[1, 128]], POS, 0)
+    iota(V("pn"), [[0, 1]], -POS, -1)
+    iota(V("slb"), [[1, 3], [48, 8]], 0, 3)
+    ms(V("sdr", p=quads[1]), 0)
+    ms(V("sdr", p=halves[1]), 0)
+    send_ids(0)
+    ms(V("ez"), 0.0)
     p0 = W("pi", 0, 1)
     ts(W("pi", 1, 1), p0, 15, A.bitwise_and)
-    ts(W("pi", 2, 1), p0, 4, A.logical_shift_right)
+    ts(W("pi", 2, 1), p0, 112, A.bitwise_and)
     ts(W("pi", 3, 1), p0, 31, A.bitwise_and)
     ts(W("pi", 4, 1), p0, 5, A.logical_shift_right, 1, A.bitwise_and)
     ts(W("pi", 5, 1), p0, 6, A.logical_shift_right)
-    ms(V("rs3", 0, 9, 3), 9 * NEG)
+    ms(V("nk"), -BIG)
     cp(W("pf", 0, 6), W("pi", 0, 6))
-    pf, r16, grp, u32c, odd, upper = [W("pf", i, 1) for i in range(6)]
-    ms(V("ma", 192, 2 * SEG, SEG), 0.0)
-    ms(V("ma", 193, 2 * SEG, SEG), 0.0)
-    ms(W("mb", 192, 2), 0.0)
-    ms(W("mb", SEG + 192, 2), 0.0)
-    ts(W("gl0", 5, 1), pf, 4.0, A.mult, float(POS + 3), A.add)
-    ts(W("gl0", 1, 1), r16, 3.0, A.is_ge, 21.0, A.mult)
-    ts(W("gl0", 2, 1), r16, 6.0, A.is_ge, 21.0, A.mult)
-    ts(W("gl0", 3, 1), grp, 3.0, A.mult, r16, A.add)
+    pf, r16, g16, u32c, odd, upper, g48, nr, fx, f16 = [W("pf", i, 1) for i in range(10)]
+    act(V("ea"), W("val", 0, 128), AF.Abs, bias=V("pn"))
+    act(V("ez", 3, 515, 4), V("ea"), AF.Relu, bias=1.0, scale=-1.0)
     for a in quads:
         cp(V("sdl", p=a), W("sdr", 0, 2, (0, 32)))
-    ts(W("gl0", 0, 1), W("gl0", 1, 1), W("gl0", 2, 1), A.add, W("gl0", 3, 1), A.add)
-    ts(W("ids", 6, 2), V("sdl"), float(P * rank), A.add)
-    send_ids(0)
-    iota(V("slb"), [[1, 3], [48, 8]], 0, 0)
-    iota(V("jj"), [[1, 3]], P * rank, 3)
-    ts(W("gl", 0, 1), W("gl0", 0, 1), 71.0, A.min)
-    for i in range(3):
-        act(W("spot", 520 * i, 520), V("val"), bias=float(POS - 1 - 520 * i), scale=-1.0)
-    for c in range(3):
-        act(W("gg", 80 * c + 48, 32), W("z80", 0, 32), bias=NEG)
-        act(W("zw", WIN * c, POS), W("z80", 0, POS), bias=NEG)
+    iota(V("iz"), [[0, 4], [1, 16], [0, 3]], 0, 0)
+    iota(V("i3"), [[16, 3]], LEAD + P * rank, 0)
+    iota(V("dio"), [[-(1 << SH), 3]], CAND, -(3 << SH))
+    act(g48, g16, scale=3.0)
+    act(W("gl0", 1, 1), r16, AF.Sign, bias=-2.5)
+    act(W("gl0", 2, 1), r16, AF.Sign, bias=-5.5)
+    act(W("gl0", 3, 1), g16, bias=r16, scale=3.0 / 16)
+    act(nr, r16, scale=-2 * BIG)
+    act(W("spot", SPW, 128), W("val", 0, 128), scale=-1.0)
+    act(W("gl0", 4, 1), W("gl0", 1, 1), bias=W("gl0", 3, 1), scale=10.5)
+    act(W("spot", SPW + 128, 128), W("val", 0, 128), scale=-1.0, bias=-128.0)
+    act(W("gl0", 0, 1), W("gl0", 2, 1), bias=W("gl0", 4, 1), scale=10.5)
+    for n in (256, 512):
+        act(W("spot", SPW + n, n), W("spot", SPW, n), bias=float(-n))
+    ms(V("rs"), 1.0)
+    ts(V("sl"), V("slb"), g48, A.subtract)
     for b in range(4):
-        act(W("hf", WIN * b, POS), W("z80", 0, POS))
-    ts(V("ez"), W("val", 0, 516), W("gl0", 5, 1), A.is_equal)
-    for a in quads:
-        cp(V("nbf", p=a), V("nbr", p=(0, 32)))
-    quant("eq", 0, 128, W("ez", 3, 512))
-    cp(V("n9"), ind(V("nbf"), W("gl", 0, 1)))
-    quant("eq", 128, 128, W("ez", 2, 512))
-    ts(V("n9a"), V("n9"), 0.0, A.is_lt, float(NONE + 1), A.mult)
-    quant("eq", 256, 128, W("ez", 1, 512))
-    tt(V("n9b"), V("n9a"), V("n9"), A.add)
-    quant("eq", 384, 128, W("ez", 0, 512))
-    cp(V("n9u"), V("n9b"))
-    ts(V("mz"), V("iz"), r16, A.not_equal, 2 * NEG, A.mult)
-    ts(W("gl0", 4, 1), r16, 3.0, A.mult)
-    quant("first", 0, P, V("xs"))
-    cp(u32(W("new0", 0, 32)), ind(u32(V("first")), V("sdl")))
-    act(W("new0s", 0, 32), ind(V("firsts"), V("sdl")), AF.Copy)
+        quant("eq", 128 * b, 128, W("ez", 3 - b, 512))
+    ms(V("rs", 0, 64, 16), 0.0)
+    quant("first", X0, P, W("xs", 0, 4 * P))
+    ts(W("gl", 0, 1), W("gl0", 0, 1), 21.0, A.add, 71.0, A.min)
+    cp(u32(W("new0", 0, 32)), ind(u32(W("first", X0, P)), V("sdl")))
+    act(W("new0s", 0, 32), ind(W("firsts", X0, P), V("sdl")), AF.Copy)
     send_cols(0)
-    iota(V("x32"), [[0, 3], [1, 32]], 0, 0)
-    iota(V("js"), [[1 << SH, 3]], 0, 3 << SH)
+    iota(W("x32", 0, 96), [[0, 3], [1, 32]], 0, 0)
+    iota(W("x32", 96, 9), [[-60, 3], [0, 3]], 119, 0)
+    iota(V("ne"), [[0, 12 * R]], 1, 0)
+    iota(V("ma", 0, 5 * SEG + 2, SEG), [[0, 6]], 0, 0)
+    iota(V("ma", 1, 5 * SEG + 2, SEG), [[0, 6]], 0, 0)
+    iota(V("ne", 0, 12 * R, 4), [[0, 3 * R]], 0, 0)
+    iota(V("nbs", 63, 192, 64), [[0, 3]], -LEAD, 0)
     iota(V("slots"), [[16, 2], [0, 6], [1, 16]], 0, 0)
-    iota(V("w16"), [[16, 24]], -(P + MID), 0)
-    iota(V("fv"), [[128, 4], [0, 2], [1, 32]], -MID, 0)
-    iota(V("fr", 0, 2 * P), [[0, 2 * P]], -1024, 0)
-    ts(V("sl"), V("slb"), W("gl0", 4, 1), A.add)
-    tt(V("gz"), ind(V("spot", 0, SPW), W("n9u", 0, 9)), V("mz"), A.add)
+    iota(V("hf", 0, 4 * WIN, WIN), [[0, 4]], 0, 0)
+    iota(V("pas"), [[0, 3]], -1, 0)
+    iota(W("val", 128, 392), [[1, 392]], POS + 128, 0)
+    iota(V("jj"), [[1, 3]], P * rank + 1, 3)
+    iota(V("fv"), [[-32, R], [1, 32]], X0 - 32 - MID, 0)
+    iota(W("fr", mine - 16, P + 32), [[1, P + 32]], X0 - 16 - MID, 0)
+    iota(V("i2"), [[256, 2]], 0, 0)
+
+    def own_entries(out, src, n, op1):
+        for c in range(3):
+            scan(W(out, 64 * c, n), W("rs", 0, n), V(src, c, 3 * n, 3), A.mult, op1)
+
+    act(W("spot", SPW + 1024, SPW - 1024), W("spot", SPW, SPW - 1024), bias=-1024.0)
+    act(V("mz"), V("iz"), AF.Abs, bias=nr, scale=2 * BIG)
+    act(V("stats"), ind(W("firsts", X0, P), V("sl")), AF.Copy)
     for b in range(4):
-        mm("pe", b, "eq", 128 * b, "first", 0, P)
-    act(V("stats"), ind(V("firsts"), V("sl")), AF.Copy)
-    for b in range(4):
-        act(W("hg", P * b, P), W("pe", 512 * b, P), scale=0.5)
-    ts(V("rs"), V("i16"), 0.0, A.is_equal, 9 * NEG, A.mult)
-    ts(V("dm"), V("i16"), r16, A.not_equal, 2 * NEG, A.mult)
+        mm("pe", b, "eq", 128 * b, "first", X0, P)
+    cp(V("nbr", p=halves[1]), V("nbr", p=halves[0]))
+    cp(u32(V("stat")), ind(u32(W("first", X0, P)), V("sl")))
+    ts(V("n9"), ind(V("nbr"), W("gl", 0, 1)), float(LEAD), A.add)
+    tt(V("gz"), ind(W("spot", SPW, SPW), W("n9", 0, 9)), W("mz", 0, 144), A.add)
+    ts(W("n9", 9, 3), V("i3"), g48, A.add, r16, A.add)
+    cp(ind(W("spot", mine, P), V("sdl")), W("val", 0, 32))
+    own_entries("nbs", "gz", 48, A.min)
+    act(V("dm"), V("iz", 0, 144, 3), AF.Abs, bias=nr, scale=2 * BIG)
     for c in range(3):
-        scan(W("nbs", 48 * c, 48), W("rs", 0, 48), V("gz", c, 144, 3), A.add, A.max)
-    cp(W("nbu", 9, 3), V("jj"))
-    for k in range(M):
-        ts(V("nbu", k, 9, 3), V("nbs", 16 * k + 15, 144, 48), -1.0, A.mult, -1.0, A.add)
-    cp(u32(V("stat")), ind(u32(V("first")), V("sl")))
-    cp(ind(V("spot"), W("ids", 6, 8)), W("val", 0, 128))
+        act(W("gg", 80 * c + 48, 32), W("nk", 0, 32), scale=2.0)
+    act(V("zw", 0, 3 * WIN, WIN), W("nk", 0, 3))
+    for b in range(3):
+        act(W("hg", P * b, P), W("pe", 512 * b, P), scale=0.5)
+
+    def caps(fixed):
+        for c in range(3):
+            act(W("cap", 80 * c, 80), V("nk"), bias=BIG / 2, scale=W(fixed[0], fixed[1] + c, 1))
 
     def products(t):
         for o in range(O):
-            mm("pz", o, "wq", 128 * o, "fw", NEW[t + 1][1] - 96, 128)
+            mm("pe", 2 + o, "wq", 128 * o, "first", X0 - 32 - 32 * t, 128)
         for o in range(O):
-            act(W("yb", 64 * t + 32 * o, 32), W("pz", 512 * o + 96, 32))
+            act(W("yb", 64 * t + 32 * o, 32), W("pe", 512 * (2 + o), 32))
 
     def place_y(t, o):
         cp(ind(V("ys%d" % o), W("ids", 16 * t + 22, 2)), W("yb", 64 * t + 32 * o, 32))
 
-    def parents():
+    def parents(num, k):
         for c in range(3):
-            act(W("pas", c, 1), W("pg", 3 * c + 2, 1), bias=W("pas", c, 1), scale=W("tk2", c, 1))
+            act(W("pas", c, 1), num(c), bias=W("pas", c, 1), scale=W("tk", 3 * k + c, 1))
+
+    def taken(t):
+        scan(W("pg", 12 * t, 12), W("ne", 12 * t, 12), V("dn"), A.mult, A.add)
+
+    def adopt(t):
+        parents(lambda c: W("pg", 12 * t + 4 * c + 3, 1), t)
 
     def mark(t):
-        cp(ind(V("fr"), V("fo")), W("fv", 64 * t, 64))
+        cp(ind(V("fr"), W("ids", 16 * t + 22, 2)), W("fv", 32 * t, 32))
+
+    odds = [lambda: ts(W("tri", 0, 99), W("x32", 0, 99), u32c, A.is_gt, odd, A.subtract),
+            lambda: ts(W("tri", 99, 6), W("x32", 99, 6), u32c, A.is_gt, upper, A.subtract),
+            lambda: tt(W("dn", 0, 11), V("nbs", 31, 192, 16), V("nbs", 15, 176, 16), A.subtract),
+            lambda: ts(W("pi", 6, 1), p0, 1, A.bitwise_and),
+            lambda: ts(W("pi", 7, 1), p0, 4, A.logical_shift_right, 1, A.bitwise_and),
+            lambda: cp(W("gl0", 4, 2), W("pi", 6, 2)),
+            lambda: ts(fx, W("gl0", 4, 1), W("gl0", 5, 1), A.not_equal, float(P + 16), A.mult),
+            lambda: ts(f16, r16, 16.0, A.mult, fx, A.add),
+            lambda: ts(V("fl"), V("i2"), f16, A.add, float(2 * P + 31), A.min),
+            lambda: place_y(2, 0),
+            lambda: place_y(2, 1)]
+
+    def fill():
+        if odds:
+            odds.pop(0)()
 
     for t in range(R):
         last = t == R - 1
         nm, a0 = NEW[t]
-        n = 12 if t == 0 else 9
-        if t > 0:
+        n = 64 if t == 0 else 48
+        if t == 0:
+            for a in quads:
+                cp(V("sdu", p=a), W("sda", 2, 6, (0, 32)))
+            for d in range(1, N):
+                cp(ind(W("spot", SPW + LEAD + P * ((rank + d) % N), P), W("sdu", 2 * d - 2, 2)), W("val", 32 * d, 32))
+        else:
             cp(ind(V("spot"), W("ids", 16 * t + 8, 6)), W("val", 128 * t + 32, 96))
-        tt(W("g2", 0, 16 * n), ind(V("spot", 0, SPW), W("nbu", 0, n)), W("dm", 0, 16 * n), A.add)
+        fill()
+        tt(W("g2", 0, 3 * n), ind(W("spot", SPW, SPW), W("n9", 0, 3 * n // 16)), W("mz", 0, 3 * n), A.subtract)
+        fill()
+        own_entries("sp", "g2", n, A.max)
+        cp(W("off", 0, 3), V("sp", 15, 48, 16))
         if t == 0:
-            ts(V("tri0"), V("x32"), u32c, A.is_gt, odd, A.subtract)
-        scan(W("sp", 0, 16 * n), W("rs", 0, 16 * n), W("g2", 0, 16 * n), A.add, A.max)
+            ts(W("tk", 12, 3), V("sp", 63, 192, 64), 0.0, A.is_gt)
+            caps(("tk", 12))
+        cp(W("off", 4, 7), V("sp", 79, 176, 16))
         if t == 0:
-            cp(V("nbc"), V("nbu"))
-            ts(V("uu"), V("sp", 159, 192, 16), 0.0, A.is_lt)
-            ts(W("tri", 0, 96), V("tri0"), STEP, A.mult)
-        for c in range(3):
-            ts(W("off", 4 * c, 3), V("sp", 48 * c + 15, 48 * c + 48, 16), W("uu", c, 1), A.mult, 0.0, A.max)
-        for c in range(3):
-            act(W("p8", 3 * c, 3), V("sp", 48 * c + 15, 48 * c + 48, 16), AF.Relu, scale=W("uu", c, 1))
-        if t == 0:
-            for c in range(3):
-                ts(V("tri", 96 + c, 102, 3), W("pf", 4, 2), -STEP, A.mult, STEP, A.add)
-            ts(W("tri", 102, 3), W("z80", 0, 3), upper, A.subtract, STEP, A.mult)
-        if t == 1:
-            quant("wq", 0, 128 * O, V("ws"))
-        if t == 2:
-            place_y(0, 0)
-            place_y(0, 1)
-        if t == 3:
-            quant("fw", 0, P, V("xs"))
-        scan(V("t2"), V("rs3"), V("p8"), A.add, A.max)
-        tt(V("t4"), V("p8", 2, 9, 3), V("js"), A.add)
-        tt(W("dd", 0, 8), W("p8", 0, 8), W("p8", 1, 8), A.subtract)
-        ts(V("t5"), V("t2", 2, 9, 3), 1.0, A.is_lt, float(EMPTY << SH), A.mult)
-        ts(V("thr"), V("t2", 2, 9, 3), 1.0, A.is_ge, float(K), A.mult)
-        if t > 1:
-            place_y(t - 1, 0)
-        tt(V("dd", 2, 9, 3), V("t4"), V("t5"), A.add)
-        if t > 1:
-            place_y(t - 1, 1)
+            cp(V("sp", 63, 192, 64), V("dio"))
+        else:
+            tt(W("dd", 0, 11), V("sp", 15, 176, 16), V("sp", 31, 192, 16), A.subtract)
         for c in range(3):
             mm("pz", c, "stat", 128 * c, nm, a0, 128)
-        for b in range(4):
+        for b in range(3 if t == 0 else 4):
             mm("pe", b, "eq", 128 * b, nm, a0, 128)
-        for c in range(3):
-            act(W("zw", WIN * c + POS + 128 * t, 128), W("pz", 512 * c, 128), bias=TINY)
+        e = 32 if t else 0
+        ts(W("zw", POS + 128 * t + e, 128 - e), W("pz", e, 128 - e), TINY, A.add)
+        for c in range(1, 3):
+            act(W("zw", WIN * c + POS + 128 * t + e, 128 - e), W("pz", 512 * c + e, 128 - e), bias=TINY)
 
         def gather(c):
-            tt(W("gg", 80 * c, 48), ind(W("zw", WIN * c, POS + 128 * t + 128), W("off", 4 * c, 3)), W("dm", 0, 48), A.add)
+            tt(W("gg", 80 * c, 48), ind(W("zw", WIN * c, POS + 128 * t + 128), W("off", 4 * c, 3)), V("dm"), A.subtract)
 
         def best(c):
-            scan(V("bb", c, 240, 3), V("z80"), W("gg", 80 * c, 80), A.add, A.max, 9 * NEG)
+            scan(V("bb", c, 240, 3), W("gg", 80 * c, 80), W("cap", 80 * c, 80), A.max, A.min, -8 * BIG)
         gather(0)
         gather(1)
         best(0)
         gather(2)
         best(1)
+        if t == 0:
+            tt(W("dd", 0, 11), V("sp", 15, 176, 16), V("sp", 31, 192, 16), A.subtract)
         best(2)
+        fill()
         vc = [W("bb", 141 + c, 1) for c in range(3)]
         hi = lambda c, h: W("ee", 96 + 3 * h + c, 1)
-        for c in range(4):
-            if c < 3:
-                act(W("ab", c, 1), vc[c], AF.Abs)
+        for c in range(3):
+            act(W("ab", c, 1), vc[c], AF.Abs, scale=STEP)
             if c > 0:
                 act(V("ee", c - 1, 105, 3), V("tri", c - 1, 105, 3), bias=vc[c - 1], scale=W("ab", c - 1, 1))
-        tr(W("rr", 384, 96), W("bb", 144, 96))
-        tt(V("ne", 1, 9, 3), W("bb", 45, 3), W("bb", 141, 3), A.is_equal)
-        cp(W("rr", 96, 96, quads[0]), W("rr", 384, 96, quads[1]))
-        cp(W("rr", 96, 96, quads[1]), W("rr", 384, 96, quads[0]))
-        act(W("rr", 96, 96, quads[2]), W("rr", 384, 96, quads[3]))
-        act(W("rr", 96, 96, quads[3]), W("rr", 384, 96, quads[2]))
+        act(V("ee", 2, 105, 3), V("tri", 2, 105, 3), bias=vc[2], scale=W("ab", 2, 1))
+        tr(W("rr", 192, 96), W("bb", 144, 96))
+        tt(V("ne", 12 * t + 1, 12 * t + 12, 4), W("bb", 45, 3), W("bb", 141, 3), A.is_equal)
+        tt(V("ne", 12 * t + 2, 12 * t + 12, 4), W("bb", 93, 3), W("bb", 141, 3), A.is_equal)
+        cp(W("rr", 96, 96, quads[0]), W("rr", 192, 96, quads[1]))
+        cp(W("rr", 96, 96, quads[1]), W("rr", 192, 96, quads[0]))
+        act(W("rr", 96, 96, quads[2]), W("rr", 192, 96, quads[3]))
+        act(W("rr", 96, 96, quads[3]), W("rr", 192, 96, quads[2]))
         tr(W("rr", 0, 96), W("ee", 0, 96))
+        if t == 0:
+            iota(V("dn", 3, 12, 4), [[0, 3]], 0, 0)
         for h in range(2):
-            act(W("rr", 192, 96, halves[h]), W("rr", 384, 96, halves[1 - h]))
+            act(W("rr", 384, 96, halves[h]), W("rr", 192, 96, halves[1 - h]))
         for h in range(2):
             act(W("rr", 288, 96, halves[h]), W("rr", 96, 96, halves[1 - h]))
-        act(V("sg"), W("rr", 192, 192), AF.Sign, bias=hi(2, 2), scale=-1.0)
+        act(V("sg"), W("rr", 288, 192), AF.Sign, bias=hi(2, 2), scale=-1.0)
         act(V("sh"), V("sg"), AF.Relu, scale=-1.0, acc=V("cnt"))
-        tt(V("ne", 2, 9, 3), W("bb", 93, 3), W("bb", 141, 3), A.is_equal)
-        ts(W("ma", SEG + 192, 1), vc[0], vc[1], A.is_equal)
+        tt(V("ma", SEG, 3 * SEG + 1, SEG), V("bb", 141, 147, 2), V("bb", 142, 148, 2), A.is_equal)
+        ts(V("dd", 3, 12, 4), W("bb", 141, 3), -BIG / 4, A.is_ge, float(CAND), A.mult)
 
-        def ahead(row, c, h):
-            ts(W(row, SEG * c, 192), W("rr", 192 * h, 192), hi(c, h), A.is_ge)
+        def ahead(c, h):
+            a = SEG * c + 2 if h == 0 else 3 * SEG + 2 + SEG * c
+            ts(W("ma", a, 192), W("rr", 288 * h, 192), hi(c, h), A.is_ge)
 
         def rank_of(c):
-            scan(W("rk", SEG * c, SEG), W("ma", SEG * c, SEG), W("mb", SEG * c, SEG), A.add, A.add)
-            act(W("rkf", 288 + c, 1), W("rk", SEG * c + SEG - 1, 1))
-        ahead("ma", 0, 0)
-        ahead("ma", 1, 0)
-        ahead("mb", 0, 1)
-        ts(W("ma", 2 * SEG + 192, 2), W("bb", 141, 2), vc[2], A.is_equal)
-        ahead("mb", 1, 1)
+            scan(W("rk", SEG * c, SEG), W("ma", SEG * c, SEG), W("ma", 3 * SEG + 2 + SEG * c, SEG), A.add, A.add)
+            act(W("rkf", 291 + c, 1), W("rk", SEG * c + SEG - 1, 1))
+
+        def slot_of(c):
+            ts(V("aa", c, 192, 3), V("slots", c, 192, 3), W("rkf", 291 + c, 1), A.is_equal, W("pp", 4 * c + 3, 1), A.mult)
+        ahead(0, 0)
+        ahead(1, 0)
+        ahead(2, 0)
+        ahead(0, 1)
+        ahead(1, 1)
         rank_of(0)
-        ahead("ma", 2, 0)
+        scan(V("pp"), W("ne", 12 * t, 12), V("dd"), A.mult, A.add)
         rank_of(1)
-        scan(V("pp"), V("ne"), V("dd"), A.mult, A.add)
-        scan(V("rkf", 2, 291, 3), W("ma", 2 * SEG, 97), W("ma", 2 * SEG + 97, 97), A.add, A.add, V("cnt"))
+        scan(V("rkf", 2, 294, 3), W("ma", 2 * SEG, 98), W("ma", 2 * SEG + 98, 98), A.add, A.add, V("cnt"))
         for c in (0, 2, 1):
-            ts(V("aa", c, 192, 3), V("slots", c, 192, 3), W("rkf", 288 + c, 1), A.is_equal, W("pp", 3 * c + 2, 1), A.mult)
+            slot_of(c)
+        act(V("thr"), V("dd", 3, 12, 4), scale=(K - 0.5) / CAND)
+        taken(t)
+        if t == 0:
+            act(W("hg", P * 3, P), W("pe", 512 * 3, P), scale=0.5)
+            mm("pe", 3, "eq", 128 * 3, nm, a0, 128)
         for b in range(4):
             act(W("hf", WIN * b + POS + 128 * t, 128), W("pe", 512 * b, 128), scale=0.5)
-        if t == 1:
-            products(0)
-            for o in range(O):
-                mm("pz", 2 + o, "wq", 128 * o, "first", 0, P)
-                act(W("ys%d" % o, P * rank, P), W("pz", 512 * (2 + o), P))
-        if t == 0:
-            ts(V("pd"), V("jj"), 1.0, A.add)
-        tr(V("at"), V("aa"))
-        tt(V("tk2"), W("rkf", 288, 3), V("thr"), A.is_lt)
-        if t == 0:
-            tt(V("pd2"), V("pd"), V("uu"), A.mult)
-        else:
-            scan(V("pg"), V("ne"), V("dn"), A.mult, A.add)
+        for m in range(2):
+            tr(W("at", 96 * m, 96), W("aa", 96 * m, 96))
         for m in range(2):
             scan(W("wp", 96 * m, 96, halves[0]), W("at", 96 * m, 96, halves[0]), W("at", 96 * m, 96, halves[1]), A.add, A.add)
         for a in quads:
             tt(V("wy", p=a), V("wp", 95, 192, 96, p=quads[0]), V("wp", 95, 192, 96, p=quads[1]), A.add)
-
-        def ids():
-            ts(W("ids", 16 * t + 22, 2), V("wy"), 2.0 ** -SH, A.mult, float(P * rank), A.add)
-
-        def f12(i):
-            if i == 1:
-                ts(V("f1"), V("wy"), SH, A.logical_shift_right, 15, A.bitwise_and)
-            else:
-                ts(V("f2"), V("wy"), SH - 1, A.logical_shift_right)
-
-        def fo():
-            for d in range(2):
-                ts(W("fo", 2 * d, 2), V("f3"), float(16 * d), A.add)
-        ts(W("wl", 0, 2), V("wy"), 2.0 ** -SH, A.mult, float(P - 1), A.min)
+        ts(W("wl", 0, 2), V("wy"), 2.0 ** -SH, A.mult)
         ts(V("wi"), V("wy"), 1023, A.bitwise_and)
+        ts(W("ids", 16 * t + 22, 2), V("wy"), 2.0 ** -SH, A.mult, mine + 0.25, A.add)
         if not last:
-            ids()
             send_ids(t + 1)
-            tt(V("uu"), V("uu"), V("tk2"), A.subtract)
-        else:
-            f12(1)
-            f12(2)
+        tt(W("tk", 3 * t, 3), W("rkf", 291, 3), V("thr"), A.is_lt)
         for b in range(3):
             act(W("gb", 32 * b, 32), ind(W("hg", P * b, P), W("wl", 0, 2)))
-        if t > 0:
-            parents()
         cp(W("wl", 2, 2), V("wi"))
         cp(W("gb", 96, 32), ind(W("hg", P * 3, P), W("wl", 0, 2)))
+        if t == 0:
+            parents(lambda c: W("jj", c, 1), 4)
+        adopt(t)
         if last:
-            tt(V("f3"), V("f2"), V("f1"), A.subtract)
             store("y", T.pa[:], V("pas"))
-        for b in (0, 1, 3, 2):
-            tt(V("bt", 384 + b, 512, 4), ind(W("hf", WIN * b, POS + 128 * t + 128), W("wl", 2, 2)), W("gb", 32 * b, 32), A.add)
+        for b in (0, 3, 1, 2):
+            tt(V("xs", 4 * P + b, 4 * P + 128, 4), ind(W("hf", WIN * b, POS + 128 * t + 128), W("wl", 2, 2)), W("gb", 32 * b, 32),
+               A.add)
         if last:
-            fo()
+            mark(t)
         else:
-            f12(1)
-            f12(2)
-        quant("fw", NEW[t + 1][1] - 96, 128, V("bt"))
-        if not last:
+            tt(V("fxd"), W("tk", 3 * t, 3), V("fxd") if t else W("tk", 12, 3), A.add)
+            caps(("fxd", 0))
+            quant("fw", NEW[t + 1][1] - 96, 128, tile)
             send_cols(t + 1)
             cp(ind(V("spot"), W("ids", 16 * t + 22, 2)), W("val", 128 * t + 128, 32))
-            tt(V("f3"), V("f2"), V("f1"), A.subtract)
-            if t == 0:
-                tt(W("dn", 0, 8), W("nbc", 0, 8), W("nbc", 1, 8), A.subtract)
-                tt(V("pas"), V("jj"), V("pd2"), A.subtract)
-                ts(V("dn", 2, 9, 3), V("nbc", 2, 9, 3), 1.0, A.add)
-            if t == 2:
-                ts(V("jw"), V("w16"), r16, A.add)
-            fo()
-            if t == 0:
-                scan(V("pg"), V("ne"), V("dn"), A.mult, A.add)
-                parents()
-        if t > 0:
-            products(t)
-        mark(t)
+        quant("first", X0 - 128 - 32 * t, 128, tile)
+        if not last:
+            for c in range(3):
+                mm("pz", c, "stat", 128 * c, "first", X0 - 32 - 32 * t, 128)
+                act(W("zw", WIN * c + POS + 128 * t + 128, 32), W("pz", 512 * c, 32), bias=TINY)
+            mark(t)
+        if t == 0:
+            quant("wq", 0, 128 * O, V("ws"))
+            for o in range(O):
+                mm("pe", o, "wq", 128 * o, "first", X0, P)
+                act(W("ys%d" % o, mine, P), W("pe", 512 * o, P))
+        products(t)
+        if t in (1, 2):
+            place_y(t - 1, 0)
+            place_y(t - 1, 1)
 
-    ids()
-    tr(V("ft"), W("fr", 0, 2 * P))
+    tr(W("ft", 0, P), W("fr", mine, P))
+    tr(W("ft", P, P + 32), W("fr", mine - 16, P + 32))
     place_y(R - 1, 0)
-    store("y", T.y[:, 0:P], W("ys0", P * rank, P))
-    tt(V("f4"), V("ft", 0, 2 * P, 32), V("jw"), A.max)
+    store("y", T.y[:, 0:P], W("ys0", mine, P))
+    ts(V("fu"), ind(V("ft"), V("fl")), float(MID), A.add)
     place_y(R - 1, 1)
-    store("s", T.y[:, P:2 * P], W("ys1", P * rank, P))
-    ts(V("fu"), V("f4"), float(P + MID), A.add)
-    cp(u32(V("fin")), ind(u32(V("fw")), V("fu")))
-    act(V("fins"), ind(V("fws"), V("fu")), AF.Copy)
+    store("s", T.y[:, P:2 * P], W("ys1", mine, P))
+    cp(u32(V("fin")), ind(u32(V("first")), W("fu", 0, 24)))
+    act(V("fins"), ind(V("firsts"), W("fu", 0, 24)), AF.Copy)
     store("y", T.oc[:], u8(V("fin")))
     for k in range(4):
         store("s" if k % 2 else "y", T.osc[4 * k:4 * k + 4, :], V("fins", p=(32 * k, 32 * k + 4)))

from concourse.bass import DstId, RemoteDMATransfer
from concourse.mybir import dt, AluOpType, ActivationFunctionType

N, P, S, K, R, M, O = 4, 384, 32, 32, 4, 3, 2
F32, BF, I32, U16, Q4, U8 = "float32", "bfloat16", "int32", "uint16", "float8_e4m3fn_x4", "uint8"
NG = N * P
LEAD = 16
SPW = NG + LEAD
SH = 12
CAND = SPW << SH
POS = 1
WIN = 528
BIG = 2.0 ** 96
SEG = 194
TINY = 2.0 ** -80
STEP = 2.0 ** -24 * (1 + 2.0 ** -8)
X0 = 96 + 32 * R
MID = X0 + 128

_BUF = {
    BF: dict(xs=4 * P + 128, ws=512 * O, ez=516, fv=32 * R, ma=5 * SEG + 2, sg=192, sh=192, rk=2 * SEG,
             hg=4 * P, hf=4 * WIN, fr=2 * SPW + 16, ft=2 * P + 32),
    I32: dict(nbr=72, sdr=2, sda=8, pi=8, wy=2, wi=2),
    U16: dict(ids=16 * (R + 1), sdl=2, sdu=6, sl=24, gl=2, n9=16, off=12, wl=4, fl=2, fu=32),
    Q4: dict(first=X0 + P, stat=P, fw=96 + 128 * (R - 1), fin=P, wq=128 * O, eq=512, new0=128),
    U8: dict(firsts=X0 + P, stats=P, fws=96 + 128 * (R - 1), fins=P, wqs=128 * O, eqs=512, new0s=128),
    F32: dict(pf=12, pn=1, ea=128, iz=192, x32=105, dm=48, rs=64, mz=192, tri=105, nk=80, slots=192, val=520,
              jj=3, dio=3, fxd=3, cap=240, slb=24, i3=3, i2=2, gl0=6,
              spot=2 * SPW, g2=192, sp=192, gz=144, nbs=192, dn=12, dd=12, thr=3,
              zw=3 * WIN, gg=240, bb=240, ab=3, ne=12 * R, ee=105, rr=480, rkf=294, cnt=1, pp=12, aa=192, at=192, wp=192,
              pg=12 * R, pas=3, tk=15, gb=128, yb=64 * R, ys0=2 * SPW, ys1=2 * SPW),
}
SCRATCH = {n: ("sbuf", [128, w], d) for d, b in _BUF.items() for n, w in b.items()}
SCRATCH["pz"] = ("psum", [128, 512 * 4], F32)
SCRATCH["pe"] = ("psum", [128, 512 * 4], F32)

SEMAPHORES = ["cv", "cs", "ct", "cg", "sent", "lx", "lw", "lnb", "lsd", "st"] + \
    ["aid%d" % t for t in range(R)] + ["acol%d" % t for t in range(R)]

A = AluOpType
AF = ActivationFunctionType


def rank_program(g, core, T, topo):
    rank = T.rank_of(core)
    if rank is None:
        return
    Q = {"v": g.vector, "s": g.scalar, "t": g.tensor, "g": g, "y": g.sync}
    own = {"v": "cv", "s": "cs", "t": "ct", "g": "cg"}
    count = {}
    known = {q: {} for q in Q}
    log = {}

    def V(name, a=0, b=None, st=1, p=(0, 128)):
        if b is None:
            b = SCRATCH[name][1][1]
        x = T[name][p[0]:p[1], a:b:st] if st != 1 else T[name][p[0]:p[1], a:b]
        cols = range(a, b, st)
        if SCRATCH[name][0] == "psum":
            cols = range(a // 512 * 512, (b + 511) // 512 * 512)
        return (x, [(name, p, frozenset(cols))])

    def W(name, a, n, p=(0, 128)):
        return V(name, a, a + n, 1, p)

    def ind(win, offs):
        return (win[0].indirect(offs[0]), win[1] + offs[1])

    def u8(v):
        return (v[0].bitcast(dt.uint8), v[1])

    def u32(v):
        return (v[0].bitcast(dt.uint32), v[1])

    def need(q, ev):
        sem, val, clock = ev
        if known[q].get(sem, 0) >= val:
            return
        Q[q].wait_ge(T.sem[sem], val)
        known[q][sem] = val
        for k2, v2 in clock.items():
            if known[q].get(k2, 0) < v2:
                known[q][k2] = v2

    def hazards(reads, writes):
        best = {}
        for accs, wr in ((reads, False), (writes, True)):
            for name, p, cols in accs:
                ps = SCRATCH[name][0] == "psum"
                for (p2, c2, w2, ev) in log.get(name, []):
                    if (wr or w2 or ps) and p[0] < p2[1] and p2[0] < p[1] and not cols.isdisjoint(c2):
                        if ev[0] not in best or best[ev[0]][1] < ev[1]:
                            best[ev[0]] = ev
        return sorted(best.values(), key=lambda e: -sum(e[2].values()))

    def note(reads, writes, ev):
        for accs, wr in ((reads, False), (writes, True)):
            for name, p, cols in accs:
                log.setdefault(name, []).append((p, cols, wr, ev))

    def run(q, fn, outs, ins, sem=None, inc=1):
        reads, writes = [], []
        for v in ins:
            if isinstance(v, tuple):
                reads += v[1]
        for v in outs:
            writes += v[1][:1]
            reads += v[1][1:]
        for ev in hazards(reads, writes):
            need(q, ev)
        sem = sem or own[q]
        count[sem] = count.get(sem, 0) + inc
        fn().then_inc(T.sem[sem], inc)
        note(reads, writes, (sem, count[sem], dict(known[q])))

    def ap(v):
        return v[0] if isinstance(v, tuple) else v

    def ts(out, in0, s1, op0, s2=None, op1=None):
        if op1 is None:
            run("v", lambda: g.vector.tensor_scalar(out[0], in0[0], ap(s1), None, op0), [out], [in0, s1])
        else:
            run("v", lambda: g.vector.tensor_scalar(out[0], in0[0], ap(s1), ap(s2), op0, op1), [out], [in0, s1, s2])

    def tt(out, in0, in1, op):
        run("v", lambda: g.vector.tensor_tensor(out[0], in0[0], in1[0], op), [out], [in0, in1])

    def cp(out, in_):
        run("v", lambda: g.vector.tensor_copy(out[0], in_[0]), [out], [in_])

    def ms(out, c):
        run("v", lambda: g.vector.memset(out[0], c), [out], [])

    def scan(out, d0, d1, op0, op1, init=0.0):
        run("v", lambda: g.vector.tensor_tensor_scan(out[0], d0[0], d1[0], ap(init), op0, op1), [out], [d0, d1, init])

    def tr(out, in_):
        run("v", lambda: g.vector.transpose(out[0], in_[0]), [out], [in_])

    def quant(name, a, n, in_):
        out, sc = W(name, a, n), W(name + "s", a, n)
        run("v", lambda: g.vector.quantize_mx(out[0], sc[0], in_[0]), [out, sc], [in_])

    def act(out, in_, func=AF.Identity, bias=None, scale=None, acc=None):
        kw = {} if acc is None else {"accum_out": acc[0]}
        if bias is not None:
            kw["bias"] = ap(bias)
        if scale is not None:
            kw["scale"] = ap(scale)
        run("s", lambda: g.scalar.activation(out[0], in_[0], func, **kw), [out] + ([acc] if acc else []), [in_, bias, scale])

    def mm(bank, k, lhs, a, rhs, b, n):
        out, l, ls, r, rs = W(bank, 512 * k, n), W(lhs, a, 128), W(lhs + "s", a, 128), W(rhs, b, n), W(rhs + "s", b, n)
        run("t", lambda: g.tensor.matmul_mx(out[0], l[0], ls[0], r[0], rs[0], True, True), [out], [l, ls, r, rs])

    def iota(out, pattern, base, cm):
        run("g", lambda: g.iota(out[0], pattern, base, cm, allow_small_or_imprecise_dtypes=True), [out], [])

    def loads(sem, items):
        for q, out, src in items:
            Q[q].dma_start(out[0], src).then_inc(T.sem[sem], 16)
        count[sem] = 16 * len(items)
        for q, out, src in items:
            note([], out[1], (sem, count[sem], {}))

    def store(q, dst, in_):
        run(q, lambda: Q[q].dma_start(dst, in_[0]), [], [in_], sem="st", inc=16)

    NEW = [("new0", 0)] + [("fw", 96 + 128 * t) for t in range(R - 1)]
    peers = [(rank + d) % N for d in range(1, N)]
    mask = -1
    for q in peers:
        mask &= topo.mask(core, T.cores[q])
    neng = bin(mask).count("1")
    dst_ids = [DstId(rid=topo.addr(T.cores[q])[0], pnc=topo.addr(T.cores[q])[1]) for q in peers]

    def send(name, a, n, sem, cast=None, to=None):
        view = (lambda v: cast(v)) if cast else (lambda v: v)
        src = view(W(name, a, n))
        for ev in hazards(src[1], []):
            need("g", ev)
        x = RemoteDMATransfer(dst_ids=dst_ids, dma_engine_mask=mask, remote_sem=T.sem[sem], srcs=[src[0]],
                              dsts=[view(W(to or name, a + n * ((rank - q) % N), n))[0] for q in peers])
        g.remote_dma_fused([x], local_sem=T.sem.sent)
        count["sent"] = count.get("sent", 0) + neng

    def send_ids(t):
        if t == 0:
            send("sdr", 0, 2, "aid0", to="sda")
        else:
            send("ids", 16 * t + 6, 2, "aid%d" % t)

    def send_cols(t):
        send(NEW[t][0], NEW[t][1], 32, "acol%d" % t, u8)
        send(NEW[t][0] + "s", NEW[t][1], 32, "acol%d" % t)

    for t in range(R):
        nm, a = NEW[t]
        for views, sem, calls in (([W("ids", 16 * t + 8, 6) if t else W("sda", 2, 6)], "aid%d" % t, 1),
                                  ([W(nm, a + 32, 96), W(nm + "s", a + 32, 96)], "acol%d" % t, 2)):
            count[sem] = calls * (N - 1) * neng
            for v in views:
                note([], v[1], (sem, count[sem], {}))

    quads = [(32 * a, 32 * a + 32) for a in range(4)]
    halves = [(0, 64), (64, 128)]
    mine = SPW + LEAD + P * rank
    tile = W("xs", 4 * P - 384, 512)

    loads("lsd", [("y", V("sdr", 0, 2, p=(0, 16)), T.sd[:]), ("s", V("sdr", 0, 2, p=(16, 32)), T.sd[:])])
    loads("lx", [("y", W("xs", 0, 4 * P), T.x[:])])
    loads("lnb", [("ys"[a % 2], V("nbr", p=(16 * a, 16 * a + 16)), T.nb[:]) for a in range(4)])
    need("y", ("acol0", count["acol0"], {}))
    loads("lw", [("y", V("ws"), T.w[:])])

    run("g", lambda: g.iota(T.pi[:, 0:1], [[0, 1]], 0, 1), [W("pi", 0, 1)], [])
    iota(W("val", 0, 128), [[1, 128]], POS, 0)
    iota(V("pn"), [[0, 1]], -POS, -1)
    iota(V("slb"), [[1, 3], [48, 8]], 0, 3)
    ms(V("sdr", p=quads[1]), 0)
    ms(V("sdr", p=halves[1]), 0)
    send_ids(0)
    ms(V("ez"), 0.0)
    p0 = W("pi", 0, 1)
    ts(W("pi", 1, 1), p0, 15, A.bitwise_and)
    ts(W("pi", 2, 1), p0, 112, A.bitwise_and)
    ts(W("pi", 3, 1), p0, 31, A.bitwise_and)
    ts(W("pi", 4, 1), p0, 5, A.logical_shift_right, 1, A.bitwise_and)
    ts(W("pi", 5, 1), p0, 6, A.logical_shift_right)
    ms(V("nk"), -BIG)
    cp(W("pf", 0, 6), W("pi", 0, 6))
    pf, r16, g16, u32c, odd, upper, g48, nr, fx, f16 = [W("pf", i, 1) for i in range(10)]
    act(V("ea"), W("val", 0, 128), AF.Abs, bias=V("pn"))
    act(V("ez", 3, 515, 4), V("ea"), AF.Relu, bias=1.0, scale=-1.0)
    for a in quads:
        cp(V("sdl", p=a), W("sdr", 0, 2, (0, 32)))
    iota(V("iz"), [[0, 4], [1, 16], [0, 3]], 0, 0)
    iota(V("i3"), [[16, 3]], LEAD + P * rank, 0)
    iota(V("dio"), [[-(1 << SH), 3]], CAND, -(3 << SH))
    act(g48, g16, scale=3.0)
    act(W("gl0", 1, 1), r16, AF.Sign, bias=-2.5)
    act(W("gl0", 2, 1), r16, AF.Sign, bias=-5.5)
    act(W("gl0", 3, 1), g16, bias=r16, scale=3.0 / 16)
    act(nr, r16, scale=-2 * BIG)
    act(W("spot", SPW, 128), W("val", 0, 128), scale=-1.0)
    act(W("gl0", 4, 1), W("gl0", 1, 1), bias=W("gl0", 3, 1), scale=10.5)
    act(W("spot", SPW + 128, 128), W("val", 0, 128), scale=-1.0, bias=-128.0)
    act(W("gl0", 0, 1), W("gl0", 2, 1), bias=W("gl0", 4, 1), scale=10.5)
    for n in (256, 512):
        act(W("spot", SPW + n, n), W("spot", SPW, n), bias=float(-n))
    ms(V("rs"), 1.0)
    ts(V("sl"), V("slb"), g48, A.subtract)
    for b in range(4):
        quant("eq", 128 * b, 128, W("ez", 3 - b, 512))
    ms(V("rs", 0, 64, 16), 0.0)
    quant("first", X0, P, W("xs", 0, 4 * P))
    ts(W("gl", 0, 1), W("gl0", 0, 1), 21.0, A.add, 71.0, A.min)
    cp(u32(W("new0", 0, 32)), ind(u32(W("first", X0, P)), V("sdl")))
    act(W("new0s", 0, 32), ind(W("firsts", X0, P), V("sdl")), AF.Copy)
    send_cols(0)
    iota(W("x32", 0, 96), [[0, 3], [1, 32]], 0, 0)
    iota(W("x32", 96, 9), [[-60, 3], [0, 3]], 119, 0)
    iota(V("ne"), [[0, 12 * R]], 1, 0)
    iota(V("ma", 0, 5 * SEG + 2, SEG), [[0, 6]], 0, 0)
    iota(V("ma", 1, 5 * SEG + 2, SEG), [[0, 6]], 0, 0)
    iota(V("ne", 0, 12 * R, 4), [[0, 3 * R]], 0, 0)
    iota(V("nbs", 63, 192, 64), [[0, 3]], -LEAD, 0)
    iota(V("slots"), [[16, 2], [0, 6], [1, 16]], 0, 0)
    iota(V("hf", 0, 4 * WIN, WIN), [[0, 4]], 0, 0)
    iota(V("pas"), [[0, 3]], -1, 0)
    iota(W("val", 128, 392), [[1, 392]], POS + 128, 0)
    iota(V("jj"), [[1, 3]], P * rank + 1, 3)
    iota(V("fv"), [[-32, R], [1, 32]], X0 - 32 - MID, 0)
    iota(W("fr", mine - 16, P + 32), [[1, P + 32]], X0 - 16 - MID, 0)
    iota(V("i2"), [[256, 2]], 0, 0)

    def own_entries(out, src, n, op1):
        for c in range(3):
            scan(W(out, 64 * c, n), W("rs", 0, n), V(src, c, 3 * n, 3), A.mult, op1)

    act(W("spot", SPW + 1024, SPW - 1024), W("spot", SPW, SPW - 1024), bias=-1024.0)
    act(V("mz"), V("iz"), AF.Abs, bias=nr, scale=2 * BIG)
    act(V("stats"), ind(W("firsts", X0, P), V("sl")), AF.Copy)
    for b in range(4):
        mm("pe", b, "eq", 128 * b, "first", X0, P)
    cp(V("nbr", p=halves[1]), V("nbr", p=halves[0]))
    cp(u32(V("stat")), ind(u32(W("first", X0, P)), V("sl")))
    ts(V("n9"), ind(V("nbr"), W("gl", 0, 1)), float(LEAD), A.add)
    tt(V("gz"), ind(W("spot", SPW, SPW), W("n9", 0, 9)), W("mz", 0, 144), A.add)
    ts(W("n9", 9, 3), V("i3"), g48, A.add, r16, A.add)
    cp(ind(W("spot", mine, P), V("sdl")), W("val", 0, 32))
    own_entries("nbs", "gz", 48, A.min)
    act(V("dm"), V("iz", 0, 144, 3), AF.Abs, bias=nr, scale=2 * BIG)
    for c in range(3):
        act(W("gg", 80 * c + 48, 32), W("nk", 0, 32), scale=2.0)
    act(V("zw", 0, 3 * WIN, WIN), W("nk", 0, 3))
    for b in range(3):
        act(W("hg", P * b, P), W("pe", 512 * b, P), scale=0.5)

    def caps(fixed):
        for c in range(3):
            act(W("cap", 80 * c, 80), V("nk"), bias=BIG / 2, scale=W(fixed[0], fixed[1] + c, 1))

    def products(t):
        for o in range(O):
            mm("pe", 2 + o, "wq", 128 * o, "first", X0 - 32 - 32 * t, 128)
        for o in range(O):
            act(W("yb", 64 * t + 32 * o, 32), W("pe", 512 * (2 + o), 32))

    def place_y(t, o):
        cp(ind(V("ys%d" % o), W("ids", 16 * t + 22, 2)), W("yb", 64 * t + 32 * o, 32))

    def parents(num, k):
        for c in range(3):
            act(W("pas", c, 1), num(c), bias=W("pas", c, 1), scale=W("tk", 3 * k + c, 1))

    def taken(t):
        scan(W("pg", 12 * t, 12), W("ne", 12 * t, 12), V("dn"), A.mult, A.add)

    def adopt(t):
        parents(lambda c: W("pg", 12 * t + 4 * c + 3, 1), t)

    def mark(t):
        cp(ind(V("fr"), W("ids", 16 * t + 22, 2)), W("fv", 32 * t, 32))

    odds = [lambda: ts(W("tri", 0, 99), W("x32", 0, 99), u32c, A.is_gt, odd, A.subtract),
            lambda: ts(W("tri", 99, 6), W("x32", 99, 6), u32c, A.is_gt, upper, A.subtract),
            lambda: tt(W("dn", 0, 11), V("nbs", 31, 192, 16), V("nbs", 15, 176, 16), A.subtract),
            lambda: ts(W("pi", 6, 1), p0, 1, A.bitwise_and),
            lambda: ts(W("pi", 7, 1), p0, 4, A.logical_shift_right, 1, A.bitwise_and),
            lambda: cp(W("gl0", 4, 2), W("pi", 6, 2)),
            lambda: ts(fx, W("gl0", 4, 1), W("gl0", 5, 1), A.not_equal, float(P + 16), A.mult),
            lambda: ts(f16, r16, 16.0, A.mult, fx, A.add),
            lambda: ts(V("fl"), V("i2"), f16, A.add, float(2 * P + 31), A.min),
            lambda: place_y(2, 0),
            lambda: place_y(2, 1)]

    def fill():
        if odds:
            odds.pop(0)()

    for t in range(R):
        last = t == R - 1
        nm, a0 = NEW[t]
        n = 64 if t == 0 else 48
        if t == 0:
            for a in quads:
                cp(V("sdu", p=a), W("sda", 2, 6, (0, 32)))
            for d in range(1, N):
                cp(ind(W("spot", SPW + LEAD + P * ((rank + d) % N), P), W("sdu", 2 * d - 2, 2)), W("val", 32 * d, 32))
        else:
            cp(ind(V("spot"), W("ids", 16 * t + 8, 6)), W("val", 128 * t + 32, 96))
        fill()
        tt(W("g2", 0, 3 * n), ind(W("spot", SPW, SPW), W("n9", 0, 3 * n // 16)), W("mz", 0, 3 * n), A.subtract)
        fill()
        own_entries("sp", "g2", n, A.max)
        cp(W("off", 0, 3), V("sp", 15, 48, 16))
        if t == 0:
            ts(W("tk", 12, 3), V("sp", 63, 192, 64), 0.0, A.is_gt)
            caps(("tk", 12))
        cp(W("off", 4, 7), V("sp", 79, 176, 16))
        if t == 0:
            cp(V("sp", 63, 192, 64), V("dio"))
        else:
            tt(W("dd", 0, 11), V("sp", 15, 176, 16), V("sp", 31, 192, 16), A.subtract)
        for c in range(3):
            mm("pz", c, "stat", 128 * c, nm, a0, 128)
        for b in range(3 if t == 0 else 4):
            mm("pe", b, "eq", 128 * b, nm, a0, 128)
        e = 32 if t else 0
        ts(W("zw", POS + 128 * t + e, 128 - e), W("pz", e, 128 - e), TINY, A.add)
        for c in range(1, 3):
            act(W("zw", WIN * c + POS + 128 * t + e, 128 - e), W("pz", 512 * c + e, 128 - e), bias=TINY)

        def gather(c):
            tt(W("gg", 80 * c, 48), ind(W("zw", WIN * c, POS + 128 * t + 128), W("off", 4 * c, 3)), V("dm"), A.subtract)

        def best(c):
            scan(V("bb", c, 240, 3), W("gg", 80 * c, 80), W("cap", 80 * c, 80), A.max, A.min, -8 * BIG)
        gather(0)
        gather(1)
        best(0)
        gather(2)
        best(1)
        if t == 0:
            tt(W("dd", 0, 11), V("sp", 15, 176, 16), V("sp", 31, 192, 16), A.subtract)
        best(2)
        fill()
        vc = [W("bb", 141 + c, 1) for c in range(3)]
        hi = lambda c, h: W("ee", 96 + 3 * h + c, 1)
        for c in range(3):
            act(W("ab", c, 1), vc[c], AF.Abs, scale=STEP)
            if c > 0:
                act(V("ee", c - 1, 105, 3), V("tri", c - 1, 105, 3), bias=vc[c - 1], scale=W("ab", c - 1, 1))
        act(V("ee", 2, 105, 3), V("tri", 2, 105, 3), bias=vc[2], scale=W("ab", 2, 1))
        tr(W("rr", 192, 96), W("bb", 144, 96))
        tt(V("ne", 12 * t + 1, 12 * t + 12, 4), W("bb", 45, 3), W("bb", 141, 3), A.is_equal)
        tt(V("ne", 12 * t + 2, 12 * t + 12, 4), W("bb", 93, 3), W("bb", 141, 3), A.is_equal)
        cp(W("rr", 96, 96, quads[0]), W("rr", 192, 96, quads[1]))
        cp(W("rr", 96, 96, quads[1]), W("rr", 192, 96, quads[0]))
        act(W("rr", 96, 96, quads[2]), W("rr", 192, 96, quads[3]))
        act(W("rr", 96, 96, quads[3]), W("rr", 192, 96, quads[2]))
        tr(W("rr", 0, 96), W("ee", 0, 96))
        if t == 0:
            iota(V("dn", 3, 12, 4), [[0, 3]], 0, 0)
        for h in range(2):
            act(W("rr", 384, 96, halves[h]), W("rr", 192, 96, halves[1 - h]))
        for h in range(2):
            act(W("rr", 288, 96, halves[h]), W("rr", 96, 96, halves[1 - h]))
        act(V("sg"), W("rr", 288, 192), AF.Sign, bias=hi(2, 2), scale=-1.0)
        act(V("sh"), V("sg"), AF.Relu, scale=-1.0, acc=V("cnt"))
        tt(V("ma", SEG, 3 * SEG + 1, SEG), V("bb", 141, 147, 2), V("bb", 142, 148, 2), A.is_equal)
        ts(V("dd", 3, 12, 4), W("bb", 141, 3), -BIG / 4, A.is_ge, float(CAND), A.mult)

        def ahead(c, h):
            a = SEG * c + 2 if h == 0 else 3 * SEG + 2 + SEG * c
            ts(W("ma", a, 192), W("rr", 288 * h, 192), hi(c, h), A.is_ge)

        def rank_of(c):
            scan(W("rk", SEG * c, SEG), W("ma", SEG * c, SEG), W("ma", 3 * SEG + 2 + SEG * c, SEG), A.add, A.add)
            act(W("rkf", 291 + c, 1), W("rk", SEG * c + SEG - 1, 1))

        def slot_of(c):
            ts(V("aa", c, 192, 3), V("slots", c, 192, 3), W("rkf", 291 + c, 1), A.is_equal, W("pp", 4 * c + 3, 1), A.mult)
        ahead(0, 0)
        ahead(1, 0)
        ahead(2, 0)
        ahead(0, 1)
        ahead(1, 1)
        rank_of(0)
        scan(V("pp"), W("ne", 12 * t, 12), V("dd"), A.mult, A.add)
        rank_of(1)
        scan(V("rkf", 2, 294, 3), W("ma", 2 * SEG, 98), W("ma", 2 * SEG + 98, 98), A.add, A.add, V("cnt"))
        for c in (0, 2, 1):
            slot_of(c)
        act(V("thr"), V("dd", 3, 12, 4), scale=(K - 0.5) / CAND)
        taken(t)
        if t == 0:
            act(W("hg", P * 3, P), W("pe", 512 * 3, P), scale=0.5)
            mm("pe", 3, "eq", 128 * 3, nm, a0, 128)
        for b in range(4):
            act(W("hf", WIN * b + POS + 128 * t, 128), W("pe", 512 * b, 128), scale=0.5)
        for m in range(2):
            tr(W("at", 96 * m, 96), W("aa", 96 * m, 96))
        for m in range(2):
            scan(W("wp", 96 * m, 96, halves[0]), W("at", 96 * m, 96, halves[0]), W("at", 96 * m, 96, halves[1]), A.add, A.add)
        for a in quads:
            tt(V("wy", p=a), V("wp", 95, 192, 96, p=quads[0]), V("wp", 95, 192, 96, p=quads[1]), A.add)
        ts(W("wl", 0, 2), V("wy"), 2.0 ** -SH, A.mult)
        ts(V("wi"), V("wy"), 1023, A.bitwise_and)
        ts(W("ids", 16 * t + 22, 2), V("wy"), 2.0 ** -SH, A.mult, mine + 0.25, A.add)
        if not last:
            send_ids(t + 1)
        tt(W("tk", 3 * t, 3), W("rkf", 291, 3), V("thr"), A.is_lt)
        for b in range(3):
            act(W("gb", 32 * b, 32), ind(W("hg", P * b, P), W("wl", 0, 2)))
        cp(W("wl", 2, 2), V("wi"))
        cp(W("gb", 96, 32), ind(W("hg", P * 3, P), W("wl", 0, 2)))
        if t == 0:
            parents(lambda c: W("jj", c, 1), 4)
        adopt(t)
        if last:
            store("y", T.pa[:], V("pas"))
        for b in (0, 3, 1, 2):
            tt(V("xs", 4 * P + b, 4 * P + 128, 4), ind(W("hf", WIN * b, POS + 128 * t + 128), W("wl", 2, 2)), W("gb", 32 * b, 32),
               A.add)
        if last:
            mark(t)
        else:
            tt(V("fxd"), W("tk", 3 * t, 3), V("fxd") if t else W("tk", 12, 3), A.add)
            caps(("fxd", 0))
            quant("fw", NEW[t + 1][1] - 96, 128, tile)
            send_cols(t + 1)
            cp(ind(V("spot"), W("ids", 16 * t + 22, 2)), W("val", 128 * t + 128, 32))
        quant("first", X0 - 128 - 32 * t, 128, tile)
        if not last:
            for c in range(3):
                mm("pz", c, "stat", 128 * c, "first", X0 - 32 - 32 * t, 128)
                act(W("zw", WIN * c + POS + 128 * t + 128, 32), W("pz", 512 * c, 32), bias=TINY)
            mark(t)
        if t == 0:
            quant("wq", 0, 128 * O, V("ws"))
            for o in range(O):
                mm("pe", o, "wq", 128 * o, "first", X0, P)
                act(W("ys%d" % o, mine, P), W("pe", 512 * o, P))
        products(t)
        if t in (1, 2):
            place_y(t - 1, 0)
            place_y(t - 1, 1)

    tr(W("ft", 0, P), W("fr", mine, P))
    tr(W("ft", P, P + 32), W("fr", mine - 16, P + 32))
    place_y(R - 1, 0)
    store("y", T.y[:, 0:P], W("ys0", mine, P))
    ts(V("fu"), ind(V("ft"), V("fl")), float(MID), A.add)
    place_y(R - 1, 1)
    store("s", T.y[:, P:2 * P], W("ys1", mine, P))
    cp(u32(V("fin")), ind(u32(V("first")), W("fu", 0, 24)))
    act(V("fins"), ind(V("firsts"), W("fu", 0, 24)), AF.Copy)
    store("y", T.oc[:], u8(V("fin")))
    for k in range(4):
        store("s" if k % 2 else "y", T.osc[4 * k:4 * k + 4, :], V("fins", p=(32 * k, 32 * k + 4)))
    for sem, val in count.items():
        g.wait_ge(T.sem[sem], val)
